import numpy as np
import ml_dtypes


def mxq(x, axis, fmt="e4m3"):
    dtype, down = {"e4m3": (ml_dtypes.float8_e4m3fn, 7), "e5m2": (ml_dtypes.float8_e5m2, 14)}[fmt]
    v = np.moveaxis(np.asarray(x, np.float32).astype(ml_dtypes.bfloat16).astype(np.float64), axis, -1)
    blocks = v.reshape(v.shape[:-1] + (-1, 32))
    amax = np.abs(blocks).max(-1, keepdims=True)
    byte = np.maximum(np.where(amax > 0, np.frexp(amax)[1] - 1 + 127, 0) - down, 1)
    scale = np.exp2(byte - 127.0)
    codes = (blocks / scale).astype(np.float32).astype(dtype).astype(np.float64)
    return np.moveaxis((codes * scale).reshape(v.shape), -1, axis)


WIDE = False


def mx_kscale(k):
    if not WIDE:
        return np.ones(k)
    levels = np.array([10, -10, 5, -5, 0])
    if k % 512:
        return np.exp2(np.random.permutation(np.resize(levels, k // 32))).repeat(32)
    a = np.empty((k // 512, 16))
    for p in range(k // 512):
        a[p, :8] = np.random.permutation(np.resize(levels, 8))
        for g in range(8):
            far = levels[np.abs(levels - a[p, g]) >= 10]
            a[p, g + 8] = far[np.random.randint(len(far))]
    return np.exp2(a.ravel()).repeat(32)


def f64(x):
    return np.asarray(x).astype(np.float64)


def striped(idx):
    return np.tile(idx.reshape(-1, 16).T, (8, 1)).astype(np.uint16)


def unstriped(offs):
    return offs[:16].T.reshape(-1).astype(np.int64)


E2M1 = np.array([0.0, 0.5, 1.0, 1.5, 2.0, 3.0, 4.0, 6.0, -0.0, -0.5, -1.0, -1.5, -2.0, -3.0, -4.0, -6.0])


def pack_weight(w, fmt):
    k, n = w.shape
    w = f64(np.asarray(w, np.float32).astype(ml_dtypes.bfloat16)).reshape(k // 32, 32, n)
    amax = np.abs(w).max(1)
    if fmt == "e4m3":
        byte = np.frexp(amax)[1] - 1 + 127 - 7
    else:
        mant, ex = np.frexp(amax / 6.0)
        byte = np.where(mant > 0.5, ex, ex - 1) + 127
    byte = np.clip(np.where(amax > 0, byte, 1), 1, 254)
    scaled = (w * np.exp2(127.0 - byte)[:, None, :]).reshape(k, n).astype(np.float32)
    by_word = np.ascontiguousarray(scaled.reshape(k // 512, 128, 4, n).transpose(0, 1, 3, 2))
    if fmt == "e4m3":
        words = by_word.astype(ml_dtypes.float8_e4m3fn).view(np.uint8)
    else:
        c = by_word.astype(ml_dtypes.float4_e2m1fn).view(np.uint8) & 0xF
        words = (c[..., 0::2] | (c[..., 1::2] << 4)).reshape(k // 512, 128, 2 * n)
    return np.ascontiguousarray(words), np.ascontiguousarray(byte.astype(np.uint8).reshape(k // 512, 16, n))


def unpack_weight(words, scales, fmt):
    g, _, n = scales.shape
    words = np.ascontiguousarray(words).reshape(g, 128, n, -1)
    if fmt == "e4m3":
        vals = words.view(ml_dtypes.float8_e4m3fn).astype(np.float64)
    else:
        nib = np.empty((g, 128, n, 4), np.uint8)
        nib[..., 0::2] = words & 0xF
        nib[..., 1::2] = words >> 4
        vals = E2M1[nib]
    vals = vals * np.repeat(np.exp2(scales.astype(np.float64) - 127.0), 8, axis=1)[..., None]
    return vals.transpose(0, 1, 3, 2).reshape(g * 512, n)


K, T, E, C, N = 1024, 768, 6, 256, 512
M = 384


def by_expert(wq, xq):
    return np.concatenate([wq[e].T @ xq[:, e * C:(e + 1) * C] for e in range(E)], axis=1)


def setup_inputs():
    n = np.random.standard_normal
    s = mx_kscale(K)[:, None]
    v = mx_kscale(N)
    first = np.random.permutation(np.repeat(np.arange(E), T // E))
    second = (first + 1 + np.random.permutation(np.repeat(np.arange(E - 1), -(-T // (E - 1)))[:T])) % E
    while np.bincount(second, minlength=E).max() != T // E:
        load = np.bincount(second, minlength=E); hi, lo = int(load.argmax()), int(load.argmin())
        t = np.flatnonzero((second == hi) & (first != lo))[0]; second[t] = lo
    slot_token = np.empty(E * C, np.int64); pos = np.empty((2, T), np.int64); fill = np.zeros(E, np.int64)
    place = np.stack([np.random.permutation(C) for _ in range(E)])
    for r, deal in enumerate((first, second)):
        for t in np.random.permutation(T):
            e = deal[t]; j = e * C + place[e, fill[e]]; fill[e] += 1; slot_token[j] = t; pos[r, t] = j
    g = np.random.uniform(0.2, 0.8, T)
    x = pack_weight(n((K, T)) * s, "e4m3")
    return {
        "x_words": x[0],
        "x_scales": x[1],
        "w": (n((E, K, N)) / np.sqrt(K) / s[None] * v[None, None, :]).astype(np.float32),
        "wp": (n((N, M)) / np.sqrt(N) / v[:, None]).astype(np.float32),
        "gate": np.stack([np.tile(g, (N, 1)), np.tile(1.0 - g, (N, 1))]).astype(np.float32),
        "offs": striped(slot_token),
        "pos1": striped(pos[0]),
        "pos2": striped(pos[1]),
    }


def reference(x_words, x_scales, w, wp, gate, offs, pos1, pos2):
    idx = unstriped(offs)
    xq = unpack_weight(x_words, x_scales, "e4m3")[:, idx]
    y = by_expert(mxq(f64(w), 1, "e4m3"), xq)
    c = f64(gate[0]) * y[:, unstriped(pos1)] + f64(gate[1]) * y[:, unstriped(pos2)]
    return mxq(f64(wp), 0, "e4m3").T @ mxq(c, 0, "e4m3")

@@ -1,0 +1,217 @@
+from contextlib import ExitStack
+
+import concourse.mybir as mybir
+from concourse.masks import make_identity
+
+K, T, E, C, N, M = 1024, 768, 6, 256, 512, 384
+S = E * C
+FLOPS = 2 * K * N * S + 2 * N * M * T
+
+F32 = mybir.dt.float32
+BF16 = mybir.dt.bfloat16
+I32 = mybir.dt.int32
+U32 = mybir.dt.uint32
+U16 = mybir.dt.uint16
+U8 = mybir.dt.uint8
+FP8X4 = mybir.dt.float8_e4m3fn_x4
+MULT = mybir.AluOpType.mult
+
+P = 128
+PACK = 4
+K_PASS = P * PACK
+PASSES = K // K_PASS
+TILES = N // P
+GATHER = 512
+CHUNKS = [256, 256, 128, 128]
+
+
+def interleave(copy, grouped, raw, c0, c1):
+    copy(
+        out=grouped[:, c0:c1, :].rearrange("p (c i) j -> p c j i", i=4),
+        in_=raw[:, :, c0:c1].rearrange("p j (c i) -> p c j i", i=4),
+    )
+
+
+def tile_moe_nxt_lin_none_kernel(tc, x_words, x_scales, w, wp, gate, offs, pos1, pos2, out):
+    nc = tc.nc
+    with ExitStack() as ctx:
+        lists = ctx.enter_context(tc.tile_pool(name="lists", bufs=1))
+        keep = ctx.enter_context(tc.tile_pool(name="keep", bufs=1))
+        big = ctx.enter_context(tc.tile_pool(name="big", bufs=14))
+        stage = ctx.enter_context(tc.tile_pool(name="stage", bufs=3))
+        quant = ctx.enter_context(tc.tile_pool(name="quant", bufs=4))
+        pair = ctx.enter_context(tc.tile_pool(name="pair", bufs=2))
+        psum = ctx.enter_context(tc.psum_pool(name="psum", bufs=1))
+
+        offs_sb = lists.tile([P, S // 16], U16, name="offs_sb")
+        pos_sb = [lists.tile([P, T // 16], U16, name="pos_sb%d" % g) for g in range(2)]
+        x_sb = [keep.tile([P, T], I32, name="x_sb%d" % o, align_bytes=64) for o in range(PASSES)]
+        xs_sb = keep.tile([P, T], U8, name="xs_sb", align_bytes=64)
+        ident = keep.tile([P, P], F32, name="ident", align_bytes=64)
+
+        nc.vector.memset(xs_sb[:].bitcast(I32), 0)
+        nc.sync.dma_start(offs_sb[:], offs)
+        for o in range(PASSES):
+            nc.sync.dma_start(x_sb[o][:], x_words[o].rearrange("p t r -> p (t r)").bitcast(I32))
+        make_identity(nc, ident[:])
+
+        pieces = [(e, o, 0, N) for e in range(E - 1) for o in range(PASSES)]
+        pieces += [(E - 1, o, h * 256, (h + 1) * 256) for h in range(2) for o in range(PASSES)]
+        raws = []
+        for i, (e, o, c0, c1) in enumerate(pieces):
+            raw = big.tile([P, PACK, c1 - c0], F32, name="raw", tag="big", align_bytes=64)
+            nc.sync.dma_start(
+                raw[:], w[e, o * K_PASS : (o + 1) * K_PASS, c0:c1].rearrange("(p j) n -> p j n", j=PACK)
+            )
+            raws.append(raw)
+            if i == 0:
+                for q in range(4):
+                    nc.sync.dma_start(
+                        xs_sb[32 * q : 32 * q + 4 * PASSES, :].bitcast(I32),
+                        x_scales[:, 4 * q : 4 * q + 4, :].bitcast(I32),
+                    )
+            if i == 4:
+                nc.sync.dma_start(pos_sb[0][:], pos1)
+                nc.sync.dma_start(pos_sb[1][:], pos2)
+        gates = []
+        t0 = 0
+        for ci, tc_w in enumerate(CHUNKS):
+            g_sb = big.tile([P, 2, TILES, tc_w], F32, name="g_sb", tag="big", align_bytes=64)
+            nc.sync.dma_start(
+                g_sb[:].rearrange("p g r t -> p (g r) t"),
+                gate[:, :, t0 : t0 + tc_w].rearrange("g (r p) t -> p (g r) t", p=P),
+            )
+            gates.append(g_sb)
+            if ci == 0:
+                wp_raw = big.tile([P, PACK, M], F32, name="wp_raw", tag="big", align_bytes=64)
+                nc.sync.dma_start(wp_raw[:], wp.rearrange("(p j) f -> p j f", j=PACK))
+            t0 += tc_w
+
+        xg = {}
+        xsg = {}
+
+        def gather_tokens(b):
+            sl = offs_sb[:, b * GATHER // 16 : (b + 1) * GATHER // 16]
+            for o in range(PASSES):
+                xg[b, o] = keep.tile([P, GATHER], U32, name="xg%d_%d" % (b, o), align_bytes=64)
+                nc.vector.tensor_copy(xg[b, o][:], x_sb[o][:].bitcast(U32).indirect(sl))
+            xsg[b] = keep.tile([P, GATHER], U8, name="xsg%d" % b, align_bytes=64)
+            nc.vector.tensor_copy(xsg[b][:], xs_sb[:].indirect(sl))
+
+        y_sb = [keep.tile([P, S], F32, name="y_sb%d" % r, align_bytes=64) for r in range(TILES)]
+        codes = {}
+
+        def quantise_piece(i):
+            e, o, c0, c1 = pieces[i]
+            width = c1 - c0
+            grouped = stage.tile([P, width, PACK], BF16, name="grouped", align_bytes=64)
+            share = 0 if i < 4 else width * 5 // 8
+            if share:
+                interleave(nc.vector.tensor_copy, grouped, raws[i], 0, share)
+            interleave(nc.scalar.copy, grouped, raws[i], share, width)
+            wq = quant.tile([P, width], U32, name="wq", align_bytes=64)
+            ws = quant.tile([P, width], U8, name="ws", align_bytes=64)
+            nc.vector.quantize_mx(out=wq[:].bitcast(FP8X4), scales=ws[:], in_=grouped[:].rearrange("p w j -> p (w j)"))
+            codes[i] = (wq, ws)
+
+        def expert(i0):
+            e, o, c0, c1 = pieces[i0]
+            b, s0 = divmod(e * C, GATHER)
+            for r in range(c0 // P, c1 // P):
+                acc = psum.tile([P, C], F32, name="acc", tag="acc", bufs=3)
+                cols = slice(r * P - c0, (r + 1) * P - c0)
+                for o in range(PASSES):
+                    wq, ws = codes[i0 + o]
+                    nc.tensor.matmul_mx(
+                        out=acc[:],
+                        lhsT=wq[:, cols].bitcast(FP8X4),
+                        lhsT_scale=ws[:, cols],
+                        rhs=xg[b, o][:, s0 : s0 + C].bitcast(FP8X4),
+                        rhs_scale=xsg[b][4 * o :, s0 : s0 + C],
+                        start=(o == 0),
+                        stop=(o == PASSES - 1),
+                    )
+                nc.scalar.copy(out=y_sb[r][:, e * C : (e + 1) * C], in_=acc[:])
+
+        gather_tokens(0)
+        gather_tokens(1)
+        for i in range(len(pieces)):
+            quantise_piece(i)
+            if i == 1:
+                gather_tokens(2)
+            if i % PASSES == PASSES - 1:
+                expert(i - PASSES + 1)
+
+        wp_grouped = keep.tile([P, M, PACK], BF16, name="wp_grouped", align_bytes=64)
+        interleave(nc.scalar.copy, wp_grouped, wp_raw, 0, M)
+        wpq = keep.tile([P, M], U32, name="wpq", align_bytes=64)
+        wps = keep.tile([P, M], U8, name="wps", align_bytes=64)
+
+        t0 = 0
+        for ci, tc_w in enumerate(CHUNKS):
+            blocks = tc_w // P
+            prod = pair.tile([P, 2, TILES, tc_w], F32, name="prod", align_bytes=64)
+            for r in range(TILES):
+                for g in range(2):
+                    nc.vector.tensor_tensor(
+                        prod[:, g, r, :],
+                        y_sb[r][:].indirect(pos_sb[g][:, t0 // 16 : (t0 + tc_w) // 16]),
+                        gates[ci][:, g, r, :],
+                        MULT,
+                    )
+            if ci == 0:
+                for f0, f1 in ((0, 256), (256, M)):
+                    nc.vector.quantize_mx(
+                        out=wpq[:, f0:f1].bitcast(FP8X4),
+                        scales=wps[:, f0:f1],
+                        in_=wp_grouped[:, f0:f1, :].rearrange("p w j -> p (w j)"),
+                    )
+            turned = psum.tile([P, blocks, 2, P], F32, name="turned", tag="turned", bufs=1)
+            for blk in range(blocks):
+                tok = slice(blk * P, (blk + 1) * P)
+                ct = psum.tile([P, N], F32, name="ct", tag="ct", bufs=2)
+                for r in range(TILES):
+                    for g in range(2):
+                        nc.tensor.matmul(
+                            ct[:, r * P : (r + 1) * P],
+                            lhsT=prod[:, g, r, tok],
+                            rhs=ident[:],
+                            start=(g == 0),
+                            stop=(g == 1),
+                            is_transpose=True,
+                        )
+                cb = pair.tile([P, N], BF16, name="cb", align_bytes=64)
+                nc.scalar.copy(
+                    out=cb[:].rearrange("t (u p e) -> t u p e", u=2, e=2),
+                    in_=ct[:].rearrange("t (p u e) -> t u p e", u=2, e=2),
+                )
+                words = cb[:].bitcast(F32)
+                for u in range(2):
+                    nc.tensor.transpose(turned[:, blk, u, :], words[:, u * P : (u + 1) * P], ident[:])
+            cg = pair.tile([P, tc_w * PACK], BF16, name="cg", align_bytes=64)
+            nc.scalar.copy(
+                out=cg[:].bitcast(F32).rearrange("p (b t u) -> p b t u", b=blocks, u=2),
+                in_=turned[:].rearrange("p b u t -> p b t u"),
+            )
+            cq = pair.tile([P, tc_w], U32, name="cq", align_bytes=64)
+            cs = pair.tile([P, tc_w], U8, name="cs", align_bytes=64)
+            nc.vector.quantize_mx(out=cq[:].bitcast(FP8X4), scales=cs[:], in_=cg[:])
+            res = pair.tile([P, M // P, tc_w], F32, name="res", align_bytes=64)
+            per_bank = min(M // P, 512 // tc_w)
+            for f0 in range(0, M // P, per_bank):
+                count = min(per_bank, M // P - f0)
+                acc2 = psum.tile([P, count, tc_w], F32, name="acc2", tag="acc2", bufs=2)
+                for f in range(count):
+                    cols = slice((f0 + f) * P, (f0 + f + 1) * P)
+                    nc.tensor.matmul_mx(
+                        out=acc2[:, f, :],
+                        lhsT=wpq[:, cols].bitcast(FP8X4),
+                        lhsT_scale=wps[:, cols],
+                        rhs=cq[:].bitcast(FP8X4),
+                        rhs_scale=cs[:],
+                        start=True,
+                        stop=True,
+                    )
+                nc.scalar.copy(out=res[:, f0 : f0 + count, :], in_=acc2[:])
+            nc.sync.dma_start(out[:, t0 : t0 + tc_w].rearrange("(f p) t -> p f t", p=P), res[:])
+            t0 += tc_w

@@ -22,12 +22,27 @@ K_PASS = P * PACK
 PASSES = K // K_PASS
 TILES = N // P
 GATHER = 512
-CHUNKS = [256, 256, 128, 128]
+HALF = N // 2
+WHOLE = 4
+GATE_W = 256
+LAST = [128, 128, 256, 256]
+CHUNKS = ([256, 256, 256], LAST)
+STARTS = ([0, 256, 512], [sum(LAST[:c]) for c in range(len(LAST))])
+LAG = 0
+SHARE = [192, 0, 0, 0, 160, 448, 128, 0, 128, 480, 0]
+ORDER = 'x0 offs u0 xs u1 pos u2 u3 x1 u4 u5 u6 u7 u8 u9 wp a0 u10 u11 a2 b0 a1 b1 b2'
+WP_SHARE = 0
+STAGE = 6
+YEV = 'VSSSSVSSVVSS'
+CEV = 'VSSSSSSV'
+GEV = 'SSVSV'
+REV = 'SVSSS'
+QUANT = 4
 
 
 def interleave(copy, grouped, raw, c0, c1):
     copy(
-        out=grouped[:, c0:c1, :].rearrange("p (c i) j -> p c j i", i=4),
+        out=grouped.rearrange("p (c i) j -> p c j i", i=4),
         in_=raw[:, :, c0:c1].rearrange("p j (c i) -> p c j i", i=4),
     )
 
@@ -37,12 +52,15 @@ def tile_moe_nxt_lin_none_kernel(tc, x_words, x_scales, w, wp, gate, offs, pos1,
     with ExitStack() as ctx:
         lists = ctx.enter_context(tc.tile_pool(name="lists", bufs=1))
         keep = ctx.enter_context(tc.tile_pool(name="keep", bufs=1))
-        big = ctx.enter_context(tc.tile_pool(name="big", bufs=14))
-        stage = ctx.enter_context(tc.tile_pool(name="stage", bufs=3))
-        quant = ctx.enter_context(tc.tile_pool(name="quant", bufs=4))
+        wide = ctx.enter_context(tc.tile_pool(name="wide", bufs=WHOLE * PASSES))
+        narrow = ctx.enter_context(tc.tile_pool(name="narrow", bufs=(E - WHOLE) * 2 * PASSES))
+        stage = ctx.enter_context(tc.tile_pool(name="stage", bufs=STAGE))
+        quant = ctx.enter_context(tc.tile_pool(name="quant", bufs=QUANT))
         pair = ctx.enter_context(tc.tile_pool(name="pair", bufs=2))
-        psum = ctx.enter_context(tc.psum_pool(name="psum", bufs=1))
+        psum = ctx.enter_context(tc.psum_pool(name="psum", bufs=8))
 
+        mover = {"S": nc.scalar.copy, "V": nc.vector.tensor_copy}
+        prod_pool = ctx.enter_context(tc.tile_pool(name="prod_pool", bufs=3))
         offs_sb = lists.tile([P, S // 16], U16, name="offs_sb")
         pos_sb = [lists.tile([P, T // 16], U16, name="pos_sb%d" % g) for g in range(2)]
         x_sb = [keep.tile([P, T], I32, name="x_sb%d" % o, align_bytes=64) for o in range(PASSES)]
@@ -50,157 +68,185 @@ def tile_moe_nxt_lin_none_kernel(tc, x_words, x_scales, w, wp, gate, offs, pos1,
         ident = keep.tile([P, P], F32, name="ident", align_bytes=64)
 
         nc.vector.memset(xs_sb[:].bitcast(I32), 0)
-        nc.sync.dma_start(offs_sb[:], offs)
-        for o in range(PASSES):
-            nc.sync.dma_start(x_sb[o][:], x_words[o].rearrange("p t r -> p (t r)").bitcast(I32))
         make_identity(nc, ident[:])
 
-        pieces = [(e, o, 0, N) for e in range(E - 1) for o in range(PASSES)]
-        pieces += [(E - 1, o, h * 256, (h + 1) * 256) for h in range(2) for o in range(PASSES)]
-        raws = []
-        for i, (e, o, c0, c1) in enumerate(pieces):
-            raw = big.tile([P, PACK, c1 - c0], F32, name="raw", tag="big", align_bytes=64)
+        def load_w(pool, e, o, c0, c1):
+            raw = pool.tile([P, PACK, c1 - c0], F32, name="raw", tag="raw", align_bytes=64)
             nc.sync.dma_start(
                 raw[:], w[e, o * K_PASS : (o + 1) * K_PASS, c0:c1].rearrange("(p j) n -> p j n", j=PACK)
             )
-            raws.append(raw)
-            if i == 0:
+            return raw
+
+        gates = {}
+
+        def load_gate(pool, tag, h, b):
+            for g in range(2):
+                gates[h, b, g] = pool.tile([P, 2, GATE_W], F32, name="gate_sb", tag=tag, align_bytes=64)
+                nc.sync.dma_start(
+                    gates[h, b, g][:],
+                    gate[g, h * HALF : (h + 1) * HALF, b * GATE_W : (b + 1) * GATE_W].rearrange("(r p) t -> p r t", p=P),
+                )
+
+        gate_pool = ctx.enter_context(tc.tile_pool(name="gate_pool", bufs=2 * T // GATE_W))
+        plan = [[(e, o, 0, N)] for e in range(WHOLE) for o in range(PASSES)]
+        plan += [[(e, o, h * HALF, HALF) for o in range(PASSES)] for h in range(2) for e in range(WHOLE, E)]
+        units = []
+        wp_raw = keep.tile([P, PACK, M], F32, name="wp_raw", align_bytes=64)
+        for item in ORDER.split():
+            if item == "offs":
+                nc.sync.dma_start(offs_sb[:], offs)
+            elif item == "pos":
+                nc.sync.dma_start(pos_sb[0][:], pos1)
+                nc.sync.dma_start(pos_sb[1][:], pos2)
+            elif item == "xs":
                 for q in range(4):
                     nc.sync.dma_start(
                         xs_sb[32 * q : 32 * q + 4 * PASSES, :].bitcast(I32),
                         x_scales[:, 4 * q : 4 * q + 4, :].bitcast(I32),
                     )
-            if i == 4:
-                nc.sync.dma_start(pos_sb[0][:], pos1)
-                nc.sync.dma_start(pos_sb[1][:], pos2)
-        gates = []
-        t0 = 0
-        for ci, tc_w in enumerate(CHUNKS):
-            g_sb = big.tile([P, 2, TILES, tc_w], F32, name="g_sb", tag="big", align_bytes=64)
-            nc.sync.dma_start(
-                g_sb[:].rearrange("p g r t -> p (g r) t"),
-                gate[:, :, t0 : t0 + tc_w].rearrange("g (r p) t -> p (g r) t", p=P),
-            )
-            gates.append(g_sb)
-            if ci == 0:
-                wp_raw = big.tile([P, PACK, M], F32, name="wp_raw", tag="big", align_bytes=64)
+            elif item == "wp":
                 nc.sync.dma_start(wp_raw[:], wp.rearrange("(p j) f -> p j f", j=PACK))
-            t0 += tc_w
+            elif item[0] == "x":
+                o = int(item[1:])
+                nc.sync.dma_start(x_sb[o][:], x_words[o].rearrange("p t r -> p (t r)").bitcast(I32))
+            elif item[0] == "u":
+                units.append(
+                    [
+                        (load_w(wide if width == N else narrow, e, o, n0, n0 + width), e, o, n0, width)
+                        for e, o, n0, width in plan[int(item[1:])]
+                    ]
+                )
+            elif item[0] == "a":
+                load_gate(gate_pool, "gate", 0, int(item[1:]))
+            else:
+                load_gate(narrow, "raw", 1, int(item[1:]))
 
         xg = {}
         xsg = {}
 
-        def gather_tokens(b):
+        def gather_words(b, o):
+            xg[b, o] = keep.tile([P, GATHER], U32, name="xg%d_%d" % (b, o), align_bytes=64)
             sl = offs_sb[:, b * GATHER // 16 : (b + 1) * GATHER // 16]
-            for o in range(PASSES):
-                xg[b, o] = keep.tile([P, GATHER], U32, name="xg%d_%d" % (b, o), align_bytes=64)
-                nc.vector.tensor_copy(xg[b, o][:], x_sb[o][:].bitcast(U32).indirect(sl))
+            nc.vector.tensor_copy(xg[b, o][:], x_sb[o][:].bitcast(U32).indirect(sl))
+
+        def gather_scales(b):
             xsg[b] = keep.tile([P, GATHER], U8, name="xsg%d" % b, align_bytes=64)
+            sl = offs_sb[:, b * GATHER // 16 : (b + 1) * GATHER // 16]
             nc.vector.tensor_copy(xsg[b][:], xs_sb[:].indirect(sl))
 
         y_sb = [keep.tile([P, S], F32, name="y_sb%d" % r, align_bytes=64) for r in range(TILES)]
+        grouped = {}
         codes = {}
+        sums = {}
 
-        def quantise_piece(i):
-            e, o, c0, c1 = pieces[i]
-            width = c1 - c0
-            grouped = stage.tile([P, width, PACK], BF16, name="grouped", align_bytes=64)
-            share = 0 if i < 4 else width * 5 // 8
-            if share:
-                interleave(nc.vector.tensor_copy, grouped, raws[i], 0, share)
-            interleave(nc.scalar.copy, grouped, raws[i], share, width)
-            wq = quant.tile([P, width], U32, name="wq", align_bytes=64)
-            ws = quant.tile([P, width], U8, name="ws", align_bytes=64)
-            nc.vector.quantize_mx(out=wq[:].bitcast(FP8X4), scales=ws[:], in_=grouped[:].rearrange("p w j -> p (w j)"))
-            codes[i] = (wq, ws)
+        def cast(copy, i, c0, c1):
+            if i not in grouped:
+                grouped[i] = stage.tile([P, N, PACK], BF16, name="grouped", align_bytes=64)
+            at = 0
+            for raw, e, o, n0, width in units[i]:
+                a, b = max(c0, at), min(c1, at + width)
+                if a < b:
+                    interleave(copy, grouped[i][:, a:b, :], raw, a - at, b - at)
+                at += width
 
-        def expert(i0):
-            e, o, c0, c1 = pieces[i0]
+        def quantise(i, c0, c1):
+            if i not in codes:
+                codes[i] = (
+                    quant.tile([P, N], U32, name="wq", align_bytes=64),
+                    quant.tile([P, N], U8, name="ws", align_bytes=64),
+                )
+            wq, ws = codes[i]
+            nc.vector.quantize_mx(
+                out=wq[:, c0:c1].bitcast(FP8X4),
+                scales=ws[:, c0:c1],
+                in_=grouped[i][:, c0:c1, :].rearrange("p w j -> p (w j)"),
+            )
+
+        def find(e, o, r):
+            for i, unit in enumerate(units):
+                at = 0
+                for raw, ue, uo, n0, width in unit:
+                    if (ue, uo) == (e, o) and n0 <= r * P < n0 + width:
+                        return i, at + r * P - n0
+                    at += width
+
+        def multiply(e, r):
             b, s0 = divmod(e * C, GATHER)
-            for r in range(c0 // P, c1 // P):
-                acc = psum.tile([P, C], F32, name="acc", tag="acc", bufs=3)
-                cols = slice(r * P - c0, (r + 1) * P - c0)
-                for o in range(PASSES):
-                    wq, ws = codes[i0 + o]
-                    nc.tensor.matmul_mx(
-                        out=acc[:],
-                        lhsT=wq[:, cols].bitcast(FP8X4),
-                        lhsT_scale=ws[:, cols],
-                        rhs=xg[b, o][:, s0 : s0 + C].bitcast(FP8X4),
-                        rhs_scale=xsg[b][4 * o :, s0 : s0 + C],
-                        start=(o == 0),
-                        stop=(o == PASSES - 1),
-                    )
-                nc.scalar.copy(out=y_sb[r][:, e * C : (e + 1) * C], in_=acc[:])
+            acc = psum.tile([P, C], F32, name="acc", tag="bank")
+            for o in range(PASSES):
+                i, c0 = find(e, o, r)
+                wq, ws = codes[i]
+                nc.tensor.matmul_mx(
+                    out=acc[:],
+                    lhsT=wq[:, c0 : c0 + P].bitcast(FP8X4),
+                    lhsT_scale=ws[:, c0 : c0 + P],
+                    rhs=xg[b, o][:, s0 : s0 + C].bitcast(FP8X4),
+                    rhs_scale=xsg[b][4 * o :, s0 : s0 + C],
+                    start=(o == 0),
+                    stop=(o == PASSES - 1),
+                )
+            sums[e, r] = acc
 
-        gather_tokens(0)
-        gather_tokens(1)
-        for i in range(len(pieces)):
-            quantise_piece(i)
-            if i == 1:
-                gather_tokens(2)
-            if i % PASSES == PASSES - 1:
-                expert(i - PASSES + 1)
+        def unload(e, r):
+            mover[YEV[find(e, PASSES - 1, r)[0]]](out=y_sb[r][:, e * C : (e + 1) * C], in_=sums[e, r][:])
 
-        wp_grouped = keep.tile([P, M, PACK], BF16, name="wp_grouped", align_bytes=64)
-        interleave(nc.scalar.copy, wp_grouped, wp_raw, 0, M)
-        wpq = keep.tile([P, M], U32, name="wpq", align_bytes=64)
-        wps = keep.tile([P, M], U8, name="wps", align_bytes=64)
+        cb = [keep.tile([P, N], BF16, name="cb%d" % blk, align_bytes=64) for blk in range(T // P)]
+        prods = {}
 
-        t0 = 0
-        for ci, tc_w in enumerate(CHUNKS):
-            blocks = tc_w // P
-            prod = pair.tile([P, 2, TILES, tc_w], F32, name="prod", align_bytes=64)
-            for r in range(TILES):
-                for g in range(2):
-                    nc.vector.tensor_tensor(
-                        prod[:, g, r, :],
-                        y_sb[r][:].indirect(pos_sb[g][:, t0 // 16 : (t0 + tc_w) // 16]),
-                        gates[ci][:, g, r, :],
-                        MULT,
-                    )
-            if ci == 0:
-                for f0, f1 in ((0, 256), (256, M)):
-                    nc.vector.quantize_mx(
-                        out=wpq[:, f0:f1].bitcast(FP8X4),
-                        scales=wps[:, f0:f1],
-                        in_=wp_grouped[:, f0:f1, :].rearrange("p w j -> p (w j)"),
-                    )
-            turned = psum.tile([P, blocks, 2, P], F32, name="turned", tag="turned", bufs=1)
-            for blk in range(blocks):
-                tok = slice(blk * P, (blk + 1) * P)
-                ct = psum.tile([P, N], F32, name="ct", tag="ct", bufs=2)
-                for r in range(TILES):
+        def combine_gather(h, t0, width, r, g):
+            if (h, t0) not in prods:
+                prods[h, t0] = prod_pool.tile([P, 2, 2, width], F32, name="prod", align_bytes=64)
+            b, at = divmod(t0, GATE_W)
+            nc.vector.tensor_tensor(
+                prods[h, t0][:, g, r, :],
+                y_sb[2 * h + r][:].indirect(pos_sb[g][:, t0 // 16 : (t0 + width) // 16]),
+                gates[h, b, g][:, r, at : at + width],
+                MULT,
+            )
+
+        def combine_sum(h, t0, width):
+            prod = prods[h, t0]
+            for blk in range(width // P):
+                ct = psum.tile([P, HALF], F32, name="ct", tag="bank")
+                for r in range(2):
                     for g in range(2):
                         nc.tensor.matmul(
                             ct[:, r * P : (r + 1) * P],
-                            lhsT=prod[:, g, r, tok],
+                            lhsT=prod[:, g, r, blk * P : (blk + 1) * P],
                             rhs=ident[:],
                             start=(g == 0),
                             stop=(g == 1),
                             is_transpose=True,
                         )
-                cb = pair.tile([P, N], BF16, name="cb", align_bytes=64)
-                nc.scalar.copy(
-                    out=cb[:].rearrange("t (u p e) -> t u p e", u=2, e=2),
+                mover[CEV[3 * h + STARTS[h].index(t0)]](
+                    out=cb[t0 // P + blk][:].rearrange("t (u p e) -> t u p e", u=2, e=2)[:, :, h * 64 : (h + 1) * 64, :],
                     in_=ct[:].rearrange("t (p u e) -> t u p e", u=2, e=2),
                 )
-                words = cb[:].bitcast(F32)
+
+        cgs = {}
+
+        def turn(t0, width):
+            blocks = width // P
+            turned = psum.tile([P, blocks, 2, P], F32, name="turned", tag="bank")
+            for blk in range(blocks):
+                words = cb[t0 // P + blk][:].bitcast(F32)
                 for u in range(2):
                     nc.tensor.transpose(turned[:, blk, u, :], words[:, u * P : (u + 1) * P], ident[:])
-            cg = pair.tile([P, tc_w * PACK], BF16, name="cg", align_bytes=64)
-            nc.scalar.copy(
-                out=cg[:].bitcast(F32).rearrange("p (b t u) -> p b t u", b=blocks, u=2),
+            cgs[t0] = pair.tile([P, width * PACK], BF16, name="cg", align_bytes=64)
+            mover[GEV[STARTS[1].index(t0)]](
+                out=cgs[t0][:].bitcast(F32).rearrange("p (b t u) -> p b t u", b=blocks, u=2),
                 in_=turned[:].rearrange("p b u t -> p b t u"),
             )
-            cq = pair.tile([P, tc_w], U32, name="cq", align_bytes=64)
-            cs = pair.tile([P, tc_w], U8, name="cs", align_bytes=64)
-            nc.vector.quantize_mx(out=cq[:].bitcast(FP8X4), scales=cs[:], in_=cg[:])
-            res = pair.tile([P, M // P, tc_w], F32, name="res", align_bytes=64)
-            per_bank = min(M // P, 512 // tc_w)
+
+        def project(t0, width):
+            cq = pair.tile([P, width], U32, name="cq", align_bytes=64)
+            cs = pair.tile([P, width], U8, name="cs", align_bytes=64)
+            nc.vector.quantize_mx(out=cq[:].bitcast(FP8X4), scales=cs[:], in_=cgs[t0][:])
+            res = pair.tile([P, M // P, width], F32, name="res", align_bytes=64)
+            per_bank = min(M // P, 512 // width)
             for f0 in range(0, M // P, per_bank):
                 count = min(per_bank, M // P - f0)
-                acc2 = psum.tile([P, count, tc_w], F32, name="acc2", tag="acc2", bufs=2)
+                acc2 = psum.tile([P, count, width], F32, name="acc2", tag="bank")
                 for f in range(count):
                     cols = slice((f0 + f) * P, (f0 + f + 1) * P)
                     nc.tensor.matmul_mx(
@@ -212,6 +258,91 @@ def tile_moe_nxt_lin_none_kernel(tc, x_words, x_scales, w, wp, gate, offs, pos1,
                         start=True,
                         stop=True,
                     )
-                nc.scalar.copy(out=res[:, f0 : f0 + count, :], in_=acc2[:])
-            nc.sync.dma_start(out[:, t0 : t0 + tc_w].rearrange("(f p) t -> p f t", p=P), res[:])
-            t0 += tc_w
+                mover[REV[STARTS[1].index(t0)]](out=res[:, f0 : f0 + count, :], in_=acc2[:])
+            nc.sync.dma_start(out[:, t0 : t0 + width].rearrange("(f p) t -> p f t", p=P), res[:])
+
+        gather_words(0, 0)
+        gather_scales(0)
+        gather_words(0, 1)
+        fillers = []
+        for b in range(1, S // GATHER):
+            fillers += [(gather_words, b, 0), (gather_words, b, 1), (gather_scales, b)]
+        last = len(units) - 1
+        first_b = last + 1 - (E - WHOLE)
+        waiting = []
+        pending = list(STARTS[0])
+        for i in range(last):
+            cast(nc.scalar.copy, i, 0, N - SHARE[i])
+            for e, r in waiting:
+                unload(e, r)
+            waiting = []
+            now = pending[:1] if i >= first_b else []
+            pending = pending[len(now) :]
+            for t0 in now:
+                for r in range(2):
+                    for g in range(2):
+                        combine_gather(0, t0, 256, r, g)
+            cast(nc.vector.tensor_copy, i, N - SHARE[i], N)
+            if 1 <= i <= len(fillers):
+                fillers[i - 1][0](*fillers[i - 1][1:])
+            quantise(i, 0, N)
+            raw, e, o, n0, width = units[i][-1]
+            if o == PASSES - 1:
+                waiting = [(e, r) for r in range(n0 // P, (n0 + width) // P)]
+                for e, r in waiting:
+                    multiply(e, r)
+                if i == first_b - 1:
+                    for e, r in waiting:
+                        unload(e, r)
+                    waiting = []
+            for t0 in now:
+                combine_sum(0, t0, 256)
+
+        cast(nc.scalar.copy, last, 0, HALF)
+        for e, r in waiting:
+            unload(e, r)
+        for t0 in pending:
+            for r in range(2):
+                for g in range(2):
+                    combine_gather(0, t0, 256, r, g)
+        quantise(last, 0, HALF)
+        cast(nc.vector.tensor_copy, last, HALF, HALF + P)
+        cast(nc.scalar.copy, last, HALF + P, N)
+        for r in range(2):
+            quantise(last, HALF + r * P, HALF + (r + 1) * P)
+            multiply(E - 1, 2 + r)
+            unload(E - 1, 2 + r)
+        for t0 in pending:
+            combine_sum(0, t0, 256)
+
+        wp_grouped = keep.tile([P, M, PACK], BF16, name="wp_grouped", align_bytes=64)
+        if WP_SHARE < M:
+            interleave(nc.scalar.copy, wp_grouped[:, WP_SHARE:, :], wp_raw, WP_SHARE, M)
+        if WP_SHARE:
+            interleave(nc.vector.tensor_copy, wp_grouped[:, :WP_SHARE, :], wp_raw, 0, WP_SHARE)
+        wpq = keep.tile([P, M], U32, name="wpq", align_bytes=64)
+        wps = keep.tile([P, M], U8, name="wps", align_bytes=64)
+
+        t0 = 0
+        before = None
+        for ci, width in enumerate(CHUNKS[1]):
+            for r in range(2):
+                for g in range(2):
+                    combine_gather(1, t0, width, r, g)
+            if ci == LAG:
+                for f0, f1 in ((0, 256), (256, M)):
+                    nc.vector.quantize_mx(
+                        out=wpq[:, f0:f1].bitcast(FP8X4),
+                        scales=wps[:, f0:f1],
+                        in_=wp_grouped[:, f0:f1, :].rearrange("p w j -> p (w j)"),
+                    )
+            combine_sum(1, t0, width)
+            turn(t0, width)
+            if LAG == 0:
+                project(t0, width)
+            elif before:
+                project(*before)
+            before = (t0, width)
+            t0 += width
+        if LAG:
+            project(*before)

@@ -23,21 +23,14 @@ PASSES = K // K_PASS
 TILES = N // P
 GATHER = 512
 HALF = N // 2
-WHOLE = 4
+WHOLE = 3
 GATE_W = 256
-LAST = [128, 128, 256, 256]
-CHUNKS = ([256, 256, 256], LAST)
-STARTS = ([0, 256, 512], [sum(LAST[:c]) for c in range(len(LAST))])
-LAG = 0
-SHARE = [192, 0, 0, 0, 160, 448, 128, 0, 128, 480, 0]
-ORDER = 'x0 offs u0 xs u1 pos u2 u3 x1 u4 u5 u6 u7 u8 u9 wp a0 u10 u11 a2 b0 a1 b1 b2'
-WP_SHARE = 0
-STAGE = 6
-YEV = 'VSSSSVSSVVSS'
-CEV = 'VSSSSSSV'
-GEV = 'SSVSV'
-REV = 'SVSSS'
-QUANT = 4
+LAST = [256, 256, 128, 128]
+STARTS = [sum(LAST[:c]) for c in range(len(LAST))]
+ORDER = "x1 offs x0 u1 u0 xs u2 u3 u4 u5 u7 u6 u9 u10 u11 pos u8 u12 u13 wp u14 a0 u16 u15 a1 u17 u18 a2 b0 b2 b1"
+SCRIPT = "x21V c001S c000S x01V x10V x11V c011S c010S q001V q000V x02V x00V c101S q011V c110S m011P x20V c100S c201S c200S q101V q010V m010P x22V c111V q110V q100V c210S q111V c300V x12V m111P c211V c410S q211V c500S q210V q200V c400V m001P q400V q410V m100P m110P c301S q201V y011S m101P y101S m201P m400P m200P q300V c310V q310V m301P q500V y400S c510V y301S y201S q510V m210P m401P m300P m500P m000P cw1S m501P c311S cw0V y100S qw0V q301V qw1V y000V y300V c411S y501S y200S y500V m211P g000V q311V c401S m311P c501S y001S g001V y401S g002V g003V y211S q411V m310P g010V g013V g012V g011V s01P q401V y310S s00P q501V y110S g020V g023V s03P s02P y210S c511S q511V y111V m411P g021V y311S m511P e01S y010S m410P y411S g022V y410S m510P y510S s04P e04S y511S g103V s05P g100V e03S g102V e02S g110V g111V g101V s11P e11S e00S s10P g122V g112V g113V g123V s12P g120V g121V e12S e10S g131V e05S s13P t0P u0S g130V s14P g132V e13S t1P g133V qc0V s15P u1S qc1V e14S t2P p0aP e15V r0aV p0bP u2S t3P u3S p1aP r1aS p1bP r1bV o1D qc2V p2aP qc3V p3aP r0bS r2aV o2D r3aV o3D o0D"
+RING = 40
+SPLIT0 = 1
 
 
 def interleave(copy, grouped, raw, c0, c1):
@@ -52,15 +45,17 @@ def tile_moe_nxt_lin_none_kernel(tc, x_words, x_scales, w, wp, gate, offs, pos1,
     with ExitStack() as ctx:
         lists = ctx.enter_context(tc.tile_pool(name="lists", bufs=1))
         keep = ctx.enter_context(tc.tile_pool(name="keep", bufs=1))
-        wide = ctx.enter_context(tc.tile_pool(name="wide", bufs=WHOLE * PASSES))
-        narrow = ctx.enter_context(tc.tile_pool(name="narrow", bufs=(E - WHOLE) * 2 * PASSES))
-        stage = ctx.enter_context(tc.tile_pool(name="stage", bufs=STAGE))
-        quant = ctx.enter_context(tc.tile_pool(name="quant", bufs=QUANT))
+        wide = ctx.enter_context(tc.tile_pool(name="wide", bufs=WHOLE * PASSES - SPLIT0))
+        narrow = ctx.enter_context(tc.tile_pool(name="narrow", bufs=(E - WHOLE) * 2 * PASSES + 2 * SPLIT0))
+        ring_pool = ctx.enter_context(tc.tile_pool(name="ring", bufs=RING))
+        small = ctx.enter_context(tc.tile_pool(name="small", bufs=12))
         pair = ctx.enter_context(tc.tile_pool(name="pair", bufs=2))
         psum = ctx.enter_context(tc.psum_pool(name="psum", bufs=8))
 
+        def ring(shape, dtype, name):
+            return ring_pool.tile(shape, dtype, name=name, tag="ring", align_bytes=64)
+
         mover = {"S": nc.scalar.copy, "V": nc.vector.tensor_copy}
-        prod_pool = ctx.enter_context(tc.tile_pool(name="prod_pool", bufs=3))
         offs_sb = lists.tile([P, S // 16], U16, name="offs_sb")
         pos_sb = [lists.tile([P, T // 16], U16, name="pos_sb%d" % g) for g in range(2)]
         x_sb = [keep.tile([P, T], I32, name="x_sb%d" % o, align_bytes=64) for o in range(PASSES)]
@@ -70,28 +65,13 @@ def tile_moe_nxt_lin_none_kernel(tc, x_words, x_scales, w, wp, gate, offs, pos1,
         nc.vector.memset(xs_sb[:].bitcast(I32), 0)
         make_identity(nc, ident[:])
 
-        def load_w(pool, e, o, c0, c1):
-            raw = pool.tile([P, PACK, c1 - c0], F32, name="raw", tag="raw", align_bytes=64)
-            nc.sync.dma_start(
-                raw[:], w[e, o * K_PASS : (o + 1) * K_PASS, c0:c1].rearrange("(p j) n -> p j n", j=PACK)
-            )
-            return raw
-
-        gates = {}
-
-        def load_gate(pool, tag, h, b):
-            for g in range(2):
-                gates[h, b, g] = pool.tile([P, 2, GATE_W], F32, name="gate_sb", tag=tag, align_bytes=64)
-                nc.sync.dma_start(
-                    gates[h, b, g][:],
-                    gate[g, h * HALF : (h + 1) * HALF, b * GATE_W : (b + 1) * GATE_W].rearrange("(r p) t -> p r t", p=P),
-                )
-
-        gate_pool = ctx.enter_context(tc.tile_pool(name="gate_pool", bufs=2 * T // GATE_W))
         plan = [[(e, o, 0, N)] for e in range(WHOLE) for o in range(PASSES)]
-        plan += [[(e, o, h * HALF, HALF) for o in range(PASSES)] for h in range(2) for e in range(WHOLE, E)]
-        units = []
-        wp_raw = keep.tile([P, PACK, M], F32, name="wp_raw", align_bytes=64)
+        if SPLIT0:
+            plan[0] = [(0, 0, 0, HALF), (0, 0, HALF, HALF)]
+        plan = [[x] for u in plan for x in u]
+        plan += [[(e, o, h * HALF, HALF)] for h in range(2) for e in range(WHOLE, E) for o in range(PASSES)]
+        pieces = {}
+        gates = {}
         for item in ORDER.split():
             if item == "offs":
                 nc.sync.dma_start(offs_sb[:], offs)
@@ -105,244 +85,189 @@ def tile_moe_nxt_lin_none_kernel(tc, x_words, x_scales, w, wp, gate, offs, pos1,
                         x_scales[:, 4 * q : 4 * q + 4, :].bitcast(I32),
                     )
             elif item == "wp":
+                wp_raw = keep.tile([P, PACK, M], F32, name="wp_raw", align_bytes=64)
                 nc.sync.dma_start(wp_raw[:], wp.rearrange("(p j) f -> p j f", j=PACK))
             elif item[0] == "x":
                 o = int(item[1:])
                 nc.sync.dma_start(x_sb[o][:], x_words[o].rearrange("p t r -> p (t r)").bitcast(I32))
             elif item[0] == "u":
-                units.append(
-                    [
-                        (load_w(wide if width == N else narrow, e, o, n0, n0 + width), e, o, n0, width)
-                        for e, o, n0, width in plan[int(item[1:])]
-                    ]
-                )
-            elif item[0] == "a":
-                load_gate(gate_pool, "gate", 0, int(item[1:]))
+                for e, o, n0, width in plan[int(item[1:])]:
+                    pool = wide if width == N else narrow
+                    raw = pool.tile([P, PACK, width], F32, name="raw", tag="raw", align_bytes=64)
+                    nc.sync.dma_start(
+                        raw[:],
+                        w[e, o * K_PASS : (o + 1) * K_PASS, n0 : n0 + width].rearrange("(p j) n -> p j n", j=PACK),
+                    )
+                    for at in range(0, width, HALF):
+                        pieces[e, o, (n0 + at) // HALF] = (raw, at)
             else:
-                load_gate(narrow, "raw", 1, int(item[1:]))
+                h, b = "ab".index(item[0]), int(item[1:])
+                pool = narrow if h else wide
+                gates[h, b] = pool.tile([P, 2, 2, GATE_W], F32, name="gate_sb", tag="raw", align_bytes=64)
+                for g in range(2):
+                    nc.sync.dma_start(
+                        gates[h, b][:, g, :, :],
+                        gate[g, h * HALF : (h + 1) * HALF, b * GATE_W : (b + 1) * GATE_W].rearrange("(r p) t -> p r t", p=P),
+                    )
 
         xg = {}
-        xsg = {}
 
-        def gather_words(b, o):
-            xg[b, o] = keep.tile([P, GATHER], U32, name="xg%d_%d" % (b, o), align_bytes=64)
+        def gather_tokens(b, o):
             sl = offs_sb[:, b * GATHER // 16 : (b + 1) * GATHER // 16]
-            nc.vector.tensor_copy(xg[b, o][:], x_sb[o][:].bitcast(U32).indirect(sl))
-
-        def gather_scales(b):
-            xsg[b] = keep.tile([P, GATHER], U8, name="xsg%d" % b, align_bytes=64)
-            sl = offs_sb[:, b * GATHER // 16 : (b + 1) * GATHER // 16]
-            nc.vector.tensor_copy(xsg[b][:], xs_sb[:].indirect(sl))
+            if o < PASSES:
+                xg[b, o] = ring([P, GATHER], U32, "xg%d_%d" % (b, o))
+                nc.vector.tensor_copy(xg[b, o][:], x_sb[o][:].bitcast(U32).indirect(sl))
+            else:
+                xg[b, o] = ring([P, GATHER], U8, "xsg%d" % b)
+                nc.vector.tensor_copy(xg[b, o][:], xs_sb[:].indirect(sl))
 
         y_sb = [keep.tile([P, S], F32, name="y_sb%d" % r, align_bytes=64) for r in range(TILES)]
         grouped = {}
         codes = {}
+
+        def cast(key, engine, raw, at, width):
+            grouped[key] = ring([P, width, PACK], BF16, "grouped")
+            interleave(mover[engine], grouped[key][:], raw, at, at + width)
+
+        def quantise(key, source, width):
+            words = ring([P, width], U32, "wq")
+            scales = small.tile([P, width], U8, name="ws", align_bytes=64)
+            nc.vector.quantize_mx(out=words[:].bitcast(FP8X4), scales=scales[:], in_=source)
+            codes[key] = (words, scales)
+
         sums = {}
 
-        def cast(copy, i, c0, c1):
-            if i not in grouped:
-                grouped[i] = stage.tile([P, N, PACK], BF16, name="grouped", align_bytes=64)
-            at = 0
-            for raw, e, o, n0, width in units[i]:
-                a, b = max(c0, at), min(c1, at + width)
-                if a < b:
-                    interleave(copy, grouped[i][:, a:b, :], raw, a - at, b - at)
-                at += width
-
-        def quantise(i, c0, c1):
-            if i not in codes:
-                codes[i] = (
-                    quant.tile([P, N], U32, name="wq", align_bytes=64),
-                    quant.tile([P, N], U8, name="ws", align_bytes=64),
-                )
-            wq, ws = codes[i]
-            nc.vector.quantize_mx(
-                out=wq[:, c0:c1].bitcast(FP8X4),
-                scales=ws[:, c0:c1],
-                in_=grouped[i][:, c0:c1, :].rearrange("p w j -> p (w j)"),
-            )
-
-        def find(e, o, r):
-            for i, unit in enumerate(units):
-                at = 0
-                for raw, ue, uo, n0, width in unit:
-                    if (ue, uo) == (e, o) and n0 <= r * P < n0 + width:
-                        return i, at + r * P - n0
-                    at += width
-
-        def multiply(e, r):
+        def multiply(e, h, r):
             b, s0 = divmod(e * C, GATHER)
             acc = psum.tile([P, C], F32, name="acc", tag="bank")
             for o in range(PASSES):
-                i, c0 = find(e, o, r)
-                wq, ws = codes[i]
+                words, scales = codes[e, o, h]
                 nc.tensor.matmul_mx(
                     out=acc[:],
-                    lhsT=wq[:, c0 : c0 + P].bitcast(FP8X4),
-                    lhsT_scale=ws[:, c0 : c0 + P],
+                    lhsT=words[:, r * P : (r + 1) * P].bitcast(FP8X4),
+                    lhsT_scale=scales[:, r * P : (r + 1) * P],
                     rhs=xg[b, o][:, s0 : s0 + C].bitcast(FP8X4),
-                    rhs_scale=xsg[b][4 * o :, s0 : s0 + C],
+                    rhs_scale=xg[b, PASSES][4 * o :, s0 : s0 + C],
                     start=(o == 0),
                     stop=(o == PASSES - 1),
                 )
-            sums[e, r] = acc
+            sums["y", e, h, r] = acc
 
-        def unload(e, r):
-            mover[YEV[find(e, PASSES - 1, r)[0]]](out=y_sb[r][:, e * C : (e + 1) * C], in_=sums[e, r][:])
+        def unload(e, h, r, engine):
+            mover[engine](out=y_sb[2 * h + r][:, e * C : (e + 1) * C], in_=sums["y", e, h, r][:])
 
-        cb = [keep.tile([P, N], BF16, name="cb%d" % blk, align_bytes=64) for blk in range(T // P)]
+        cb = {}
         prods = {}
 
-        def combine_gather(h, t0, width, r, g):
-            if (h, t0) not in prods:
-                prods[h, t0] = prod_pool.tile([P, 2, 2, width], F32, name="prod", align_bytes=64)
+        def combine_gather(h, t0, width, k):
+            r, g = divmod(k, 2)
+            prods[h, t0, k] = ring([P, width], F32, "prod")
             b, at = divmod(t0, GATE_W)
             nc.vector.tensor_tensor(
-                prods[h, t0][:, g, r, :],
+                prods[h, t0, k][:],
                 y_sb[2 * h + r][:].indirect(pos_sb[g][:, t0 // 16 : (t0 + width) // 16]),
-                gates[h, b, g][:, r, at : at + width],
+                gates[h, b][:, g, r, at : at + width],
                 MULT,
             )
 
-        def combine_sum(h, t0, width):
-            prod = prods[h, t0]
-            for blk in range(width // P):
-                ct = psum.tile([P, HALF], F32, name="ct", tag="bank")
-                for r in range(2):
-                    for g in range(2):
-                        nc.tensor.matmul(
-                            ct[:, r * P : (r + 1) * P],
-                            lhsT=prod[:, g, r, blk * P : (blk + 1) * P],
-                            rhs=ident[:],
-                            start=(g == 0),
-                            stop=(g == 1),
-                            is_transpose=True,
-                        )
-                mover[CEV[3 * h + STARTS[h].index(t0)]](
-                    out=cb[t0 // P + blk][:].rearrange("t (u p e) -> t u p e", u=2, e=2)[:, :, h * 64 : (h + 1) * 64, :],
-                    in_=ct[:].rearrange("t (p u e) -> t u p e", u=2, e=2),
+        chunks = ([(b * GATE_W, GATE_W) for b in range(T // GATE_W)], list(zip(STARTS, LAST)))
+
+        def combine_sum(h, at):
+            t0 = max(s for s, width in chunks[h] if s <= at * P)
+            ct = psum.tile([P, HALF], F32, name="ct", tag="bank")
+            for k in range(4):
+                r, g = divmod(k, 2)
+                nc.tensor.matmul(
+                    ct[:, r * P : (r + 1) * P],
+                    lhsT=prods[h, t0, k][:, at * P - t0 : (at + 1) * P - t0],
+                    rhs=ident[:],
+                    start=(g == 0),
+                    stop=(g == 1),
+                    is_transpose=True,
                 )
+            sums["c", h, at] = ct
 
-        cgs = {}
+        def round_sum(h, at, engine):
+            if at not in cb:
+                cb[at] = ring([P, N], BF16, "cb")
+            mover[engine](
+                out=cb[at][:].rearrange("t (u p e) -> t u p e", u=2, e=2)[:, :, h * 64 : (h + 1) * 64, :],
+                in_=sums["c", h, at][:].rearrange("t (p u e) -> t u p e", u=2, e=2),
+            )
 
-        def turn(t0, width):
+        def turn(c):
+            t0, width = STARTS[c], LAST[c]
             blocks = width // P
             turned = psum.tile([P, blocks, 2, P], F32, name="turned", tag="bank")
             for blk in range(blocks):
                 words = cb[t0 // P + blk][:].bitcast(F32)
                 for u in range(2):
                     nc.tensor.transpose(turned[:, blk, u, :], words[:, u * P : (u + 1) * P], ident[:])
-            cgs[t0] = pair.tile([P, width * PACK], BF16, name="cg", align_bytes=64)
-            mover[GEV[STARTS[1].index(t0)]](
-                out=cgs[t0][:].bitcast(F32).rearrange("p (b t u) -> p b t u", b=blocks, u=2),
-                in_=turned[:].rearrange("p b u t -> p b t u"),
+            sums["t", c] = turned
+
+        def unturn(c, engine):
+            grouped["c", c] = ring([P, LAST[c] * PACK], BF16, "cg")
+            mover[engine](
+                out=grouped["c", c][:].bitcast(F32).rearrange("p (b t u) -> p b t u", t=P, u=2),
+                in_=sums["t", c][:].rearrange("p b u t -> p b t u"),
             )
 
-        def project(t0, width):
-            cq = pair.tile([P, width], U32, name="cq", align_bytes=64)
-            cs = pair.tile([P, width], U8, name="cs", align_bytes=64)
-            nc.vector.quantize_mx(out=cq[:].bitcast(FP8X4), scales=cs[:], in_=cgs[t0][:])
-            res = pair.tile([P, M // P, width], F32, name="res", align_bytes=64)
-            per_bank = min(M // P, 512 // width)
-            for f0 in range(0, M // P, per_bank):
-                count = min(per_bank, M // P - f0)
-                acc2 = psum.tile([P, count, width], F32, name="acc2", tag="bank")
-                for f in range(count):
-                    cols = slice((f0 + f) * P, (f0 + f + 1) * P)
-                    nc.tensor.matmul_mx(
-                        out=acc2[:, f, :],
-                        lhsT=wpq[:, cols].bitcast(FP8X4),
-                        lhsT_scale=wps[:, cols],
-                        rhs=cq[:].bitcast(FP8X4),
-                        rhs_scale=cs[:],
-                        start=True,
-                        stop=True,
-                    )
-                mover[REV[STARTS[1].index(t0)]](out=res[:, f0 : f0 + count, :], in_=acc2[:])
-            nc.sync.dma_start(out[:, t0 : t0 + width].rearrange("(f p) t -> p f t", p=P), res[:])
+        def project(c, part):
+            width = LAST[c]
+            cq, cs = codes["c", c]
+            first = 2 * part
+            count = min(M // P - first, 512 // width)
+            acc2 = psum.tile([P, count, width], F32, name="acc2", tag="bank")
+            for f in range(first, first + count):
+                words, scales = codes["wp", f // 2]
+                cols = slice(f % 2 * P, (f % 2 + 1) * P)
+                nc.tensor.matmul_mx(
+                    out=acc2[:, f - first, :],
+                    lhsT=words[:, cols].bitcast(FP8X4),
+                    lhsT_scale=scales[:, cols],
+                    rhs=cq[:].bitcast(FP8X4),
+                    rhs_scale=cs[:],
+                    start=True,
+                    stop=True,
+                )
+            sums["p", c, part] = (acc2, first, count)
 
-        gather_words(0, 0)
-        gather_scales(0)
-        gather_words(0, 1)
-        fillers = []
-        for b in range(1, S // GATHER):
-            fillers += [(gather_words, b, 0), (gather_words, b, 1), (gather_scales, b)]
-        last = len(units) - 1
-        first_b = last + 1 - (E - WHOLE)
-        waiting = []
-        pending = list(STARTS[0])
-        for i in range(last):
-            cast(nc.scalar.copy, i, 0, N - SHARE[i])
-            for e, r in waiting:
-                unload(e, r)
-            waiting = []
-            now = pending[:1] if i >= first_b else []
-            pending = pending[len(now) :]
-            for t0 in now:
-                for r in range(2):
-                    for g in range(2):
-                        combine_gather(0, t0, 256, r, g)
-            cast(nc.vector.tensor_copy, i, N - SHARE[i], N)
-            if 1 <= i <= len(fillers):
-                fillers[i - 1][0](*fillers[i - 1][1:])
-            quantise(i, 0, N)
-            raw, e, o, n0, width = units[i][-1]
-            if o == PASSES - 1:
-                waiting = [(e, r) for r in range(n0 // P, (n0 + width) // P)]
-                for e, r in waiting:
-                    multiply(e, r)
-                if i == first_b - 1:
-                    for e, r in waiting:
-                        unload(e, r)
-                    waiting = []
-            for t0 in now:
-                combine_sum(0, t0, 256)
-
-        cast(nc.scalar.copy, last, 0, HALF)
-        for e, r in waiting:
-            unload(e, r)
-        for t0 in pending:
-            for r in range(2):
-                for g in range(2):
-                    combine_gather(0, t0, 256, r, g)
-        quantise(last, 0, HALF)
-        cast(nc.vector.tensor_copy, last, HALF, HALF + P)
-        cast(nc.scalar.copy, last, HALF + P, N)
-        for r in range(2):
-            quantise(last, HALF + r * P, HALF + (r + 1) * P)
-            multiply(E - 1, 2 + r)
-            unload(E - 1, 2 + r)
-        for t0 in pending:
-            combine_sum(0, t0, 256)
-
-        wp_grouped = keep.tile([P, M, PACK], BF16, name="wp_grouped", align_bytes=64)
-        if WP_SHARE < M:
-            interleave(nc.scalar.copy, wp_grouped[:, WP_SHARE:, :], wp_raw, WP_SHARE, M)
-        if WP_SHARE:
-            interleave(nc.vector.tensor_copy, wp_grouped[:, :WP_SHARE, :], wp_raw, 0, WP_SHARE)
-        wpq = keep.tile([P, M], U32, name="wpq", align_bytes=64)
-        wps = keep.tile([P, M], U8, name="wps", align_bytes=64)
-
-        t0 = 0
-        before = None
-        for ci, width in enumerate(CHUNKS[1]):
-            for r in range(2):
-                for g in range(2):
-                    combine_gather(1, t0, width, r, g)
-            if ci == LAG:
-                for f0, f1 in ((0, 256), (256, M)):
-                    nc.vector.quantize_mx(
-                        out=wpq[:, f0:f1].bitcast(FP8X4),
-                        scales=wps[:, f0:f1],
-                        in_=wp_grouped[:, f0:f1, :].rearrange("p w j -> p (w j)"),
-                    )
-            combine_sum(1, t0, width)
-            turn(t0, width)
-            if LAG == 0:
-                project(t0, width)
-            elif before:
-                project(*before)
-            before = (t0, width)
-            t0 += width
-        if LAG:
-            project(*before)
+        res = [keep.tile([P, M // P, width], F32, name="res%d" % c, align_bytes=64) for c, width in enumerate(LAST)]
+        wp_parts = ((0, 256), (256, M - 256))
+        for word in SCRIPT.split():
+            kind, engine = word[0], word[-1]
+            a = [int(ch) for ch in word[1:] if ch in "0123456789"]
+            if word[:2] == "cw":
+                cast(("wp", a[0]), engine, wp_raw, *wp_parts[a[0]])
+            elif word[:2] == "qw":
+                quantise(("wp", a[0]), grouped["wp", a[0]][:].rearrange("p w j -> p (w j)"), wp_parts[a[0]][1])
+            elif word[:2] == "qc":
+                quantise(("c", a[0]), grouped["c", a[0]][:], LAST[a[0]])
+            elif kind == "c":
+                cast(tuple(a), engine, *pieces[tuple(a)], HALF)
+            elif kind == "q":
+                quantise(tuple(a), grouped[tuple(a)][:].rearrange("p w j -> p (w j)"), HALF)
+            elif kind == "x":
+                gather_tokens(*a)
+            elif kind == "m":
+                multiply(*a)
+            elif kind == "y":
+                unload(*a, engine)
+            elif kind == "g":
+                combine_gather(a[0], *chunks[a[0]][a[1]], a[2])
+            elif kind == "s":
+                combine_sum(*a)
+            elif kind == "e":
+                round_sum(*a, engine)
+            elif kind == "t":
+                turn(*a)
+            elif kind == "u":
+                unturn(*a, engine)
+            elif kind == "p":
+                project(a[0], "ab".index(word[2]))
+            elif kind == "r":
+                acc2, first, count = sums["p", a[0], "ab".index(word[2])]
+                mover[engine](out=res[a[0]][:, first : first + count, :], in_=acc2[:])
+            else:
+                t0, width = chunks[1][a[0]]
+                nc.sync.dma_start(out[:, t0 : t0 + width].rearrange("(f p) t -> p f t", p=P), res[a[0]][:])

@@ -4,8 +4,8 @@ import concourse.mybir as mybir
 from concourse.masks import make_identity
 
 K, T, E, C, N, M = 1024, 768, 6, 256, 512, 384
-S = E * C
-FLOPS = 2 * K * N * S + 2 * N * M * T
+SLOTS = E * C
+FLOPS = 2 * K * N * SLOTS + 2 * N * M * T
 
 F32 = mybir.dt.float32
 BF16 = mybir.dt.bfloat16
@@ -14,50 +14,51 @@ U32 = mybir.dt.uint32
 U16 = mybir.dt.uint16
 U8 = mybir.dt.uint8
 FP8X4 = mybir.dt.float8_e4m3fn_x4
-MULT = mybir.AluOpType.mult
 
 P = 128
 PACK = 4
 K_PASS = P * PACK
 PASSES = K // K_PASS
-TILES = N // P
-GATHER = 512
 HALF = N // 2
-WHOLE = 3
-GATE_W = 256
-LAST = [256, 256, 128, 128]
-STARTS = [sum(LAST[:c]) for c in range(len(LAST))]
-ORDER = "x1 offs x0 u1 u0 xs u2 u3 u4 u5 u7 u6 u9 u10 u11 pos u8 u12 u13 wp u14 a0 u16 u15 a1 u17 u18 a2 b0 b2 b1"
-SCRIPT = "x21V c001S c000S x01V x10V x11V c011S c010S q001V q000V x02V x00V c101S q011V c110S m011P x20V c100S c201S c200S q101V q010V m010P x22V c111V q110V q100V c210S q111V c300V x12V m111P c211V c410S q211V c500S q210V q200V c400V m001P q400V q410V m100P m110P c301S q201V y011S m101P y101S m201P m400P m200P q300V c310V q310V m301P q500V y400S c510V y301S y201S q510V m210P m401P m300P m500P m000P cw1S m501P c311S cw0V y100S qw0V q301V qw1V y000V y300V c411S y501S y200S y500V m211P g000V q311V c401S m311P c501S y001S g001V y401S g002V g003V y211S q411V m310P g010V g013V g012V g011V s01P q401V y310S s00P q501V y110S g020V g023V s03P s02P y210S c511S q511V y111V m411P g021V y311S m511P e01S y010S m410P y411S g022V y410S m510P y510S s04P e04S y511S g103V s05P g100V e03S g102V e02S g110V g111V g101V s11P e11S e00S s10P g122V g112V g113V g123V s12P g120V g121V e12S e10S g131V e05S s13P t0P u0S g130V s14P g132V e13S t1P g133V qc0V s15P u1S qc1V e14S t2P p0aP e15V r0aV p0bP u2S t3P u3S p1aP r1aS p1bP r1bV o1D qc2V p2aP qc3V p3aP r0bS r2aV o2D r3aV o3D o0D"
+STRIPE = 16
+GATHER = 512
+SCALES = PASSES
+WHOLE = 4
+
+PIECES = [(e, o, h) for e in range(WHOLE) for o in range(PASSES) for h in range(2)] + [
+    (e, o, h) for h in range(2) for e in range(WHOLE, E) for o in range(PASSES)
+]
+CLOSING = [(E - 1, PASSES - 1, h) for h in range(2)]
+ON_VECTOR = (4, 6, 9, 12, 14, 16, 18)
+TOKEN_GATHER_AT = (-1, 0, 1, 1, 2, 3, 5, 8, 11)
+FIRST_HALF_GATHERS = {21: 4, 22: 5}
+CHUNKS = ([(0, 256), (256, 256), (512, 256)], [(0, 256), (256, 256), (512, 128), (640, 128)])
+GATE_CUT = 256
+WP_PARTS = ((0, 256), (256, 128))
 RING = 40
-SPLIT0 = 1
-
-
-def interleave(copy, grouped, raw, c0, c1):
-    copy(
-        out=grouped.rearrange("p (c i) j -> p c j i", i=4),
-        in_=raw[:, :, c0:c1].rearrange("p j (c i) -> p c j i", i=4),
-    )
+PLANES = 12
 
 
 def tile_moe_nxt_lin_none_kernel(tc, x_words, x_scales, w, wp, gate, offs, pos1, pos2, out):
     nc = tc.nc
+    on_scalar, on_vector = nc.scalar.copy, nc.vector.tensor_copy
     with ExitStack() as ctx:
         lists = ctx.enter_context(tc.tile_pool(name="lists", bufs=1))
         keep = ctx.enter_context(tc.tile_pool(name="keep", bufs=1))
-        wide = ctx.enter_context(tc.tile_pool(name="wide", bufs=WHOLE * PASSES - SPLIT0))
-        narrow = ctx.enter_context(tc.tile_pool(name="narrow", bufs=(E - WHOLE) * 2 * PASSES + 2 * SPLIT0))
+        wide = ctx.enter_context(tc.tile_pool(name="wide", bufs=WHOLE * PASSES))
+        narrow = ctx.enter_context(tc.tile_pool(name="narrow", bufs=(E - WHOLE) * PASSES * 2))
         ring_pool = ctx.enter_context(tc.tile_pool(name="ring", bufs=RING))
-        small = ctx.enter_context(tc.tile_pool(name="small", bufs=12))
-        pair = ctx.enter_context(tc.tile_pool(name="pair", bufs=2))
+        planes = ctx.enter_context(tc.tile_pool(name="planes", bufs=PLANES))
         psum = ctx.enter_context(tc.psum_pool(name="psum", bufs=8))
 
         def ring(shape, dtype, name):
             return ring_pool.tile(shape, dtype, name=name, tag="ring", align_bytes=64)
 
-        mover = {"S": nc.scalar.copy, "V": nc.vector.tensor_copy}
-        offs_sb = lists.tile([P, S // 16], U16, name="offs_sb")
-        pos_sb = [lists.tile([P, T // 16], U16, name="pos_sb%d" % g) for g in range(2)]
+        def bank(shape, name):
+            return psum.tile(shape, F32, name=name, tag="bank")
+
+        offs_sb = lists.tile([P, SLOTS // STRIPE], U16, name="offs_sb")
+        pos_sb = [lists.tile([P, T // STRIPE], U16, name="pos_sb%d" % g) for g in range(2)]
         x_sb = [keep.tile([P, T], I32, name="x_sb%d" % o, align_bytes=64) for o in range(PASSES)]
         xs_sb = keep.tile([P, T], U8, name="xs_sb", align_bytes=64)
         ident = keep.tile([P, P], F32, name="ident", align_bytes=64)
@@ -65,209 +66,252 @@ def tile_moe_nxt_lin_none_kernel(tc, x_words, x_scales, w, wp, gate, offs, pos1,
         nc.vector.memset(xs_sb[:].bitcast(I32), 0)
         make_identity(nc, ident[:])
 
-        plan = [[(e, o, 0, N)] for e in range(WHOLE) for o in range(PASSES)]
-        if SPLIT0:
-            plan[0] = [(0, 0, 0, HALF), (0, 0, HALF, HALF)]
-        plan = [[x] for u in plan for x in u]
-        plan += [[(e, o, h * HALF, HALF)] for h in range(2) for e in range(WHOLE, E) for o in range(PASSES)]
-        pieces = {}
+        raw = {}
         gates = {}
-        for item in ORDER.split():
-            if item == "offs":
-                nc.sync.dma_start(offs_sb[:], offs)
-            elif item == "pos":
-                nc.sync.dma_start(pos_sb[0][:], pos1)
-                nc.sync.dma_start(pos_sb[1][:], pos2)
-            elif item == "xs":
-                for q in range(4):
-                    nc.sync.dma_start(
-                        xs_sb[32 * q : 32 * q + 4 * PASSES, :].bitcast(I32),
-                        x_scales[:, 4 * q : 4 * q + 4, :].bitcast(I32),
-                    )
-            elif item == "wp":
-                wp_raw = keep.tile([P, PACK, M], F32, name="wp_raw", align_bytes=64)
-                nc.sync.dma_start(wp_raw[:], wp.rearrange("(p j) f -> p j f", j=PACK))
-            elif item[0] == "x":
-                o = int(item[1:])
-                nc.sync.dma_start(x_sb[o][:], x_words[o].rearrange("p t r -> p (t r)").bitcast(I32))
-            elif item[0] == "u":
-                for e, o, n0, width in plan[int(item[1:])]:
-                    pool = wide if width == N else narrow
-                    raw = pool.tile([P, PACK, width], F32, name="raw", tag="raw", align_bytes=64)
-                    nc.sync.dma_start(
-                        raw[:],
-                        w[e, o * K_PASS : (o + 1) * K_PASS, n0 : n0 + width].rearrange("(p j) n -> p j n", j=PACK),
-                    )
-                    for at in range(0, width, HALF):
-                        pieces[e, o, (n0 + at) // HALF] = (raw, at)
-            else:
-                h, b = "ab".index(item[0]), int(item[1:])
-                pool = narrow if h else wide
-                gates[h, b] = pool.tile([P, 2, 2, GATE_W], F32, name="gate_sb", tag="raw", align_bytes=64)
-                for g in range(2):
-                    nc.sync.dma_start(
-                        gates[h, b][:, g, :, :],
-                        gate[g, h * HALF : (h + 1) * HALF, b * GATE_W : (b + 1) * GATE_W].rearrange("(r p) t -> p r t", p=P),
-                    )
 
-        xg = {}
+        def load_words(o):
+            nc.sync.dma_start(x_sb[o][:], x_words[o].rearrange("p t r -> p (t r)").bitcast(I32))
 
-        def gather_tokens(b, o):
-            sl = offs_sb[:, b * GATHER // 16 : (b + 1) * GATHER // 16]
-            if o < PASSES:
-                xg[b, o] = ring([P, GATHER], U32, "xg%d_%d" % (b, o))
-                nc.vector.tensor_copy(xg[b, o][:], x_sb[o][:].bitcast(U32).indirect(sl))
-            else:
-                xg[b, o] = ring([P, GATHER], U8, "xsg%d" % b)
-                nc.vector.tensor_copy(xg[b, o][:], xs_sb[:].indirect(sl))
+        def load_weights(pool, e, o, n0, width):
+            rows = pool.tile([P, PACK, width], F32, name="raw", tag="load", align_bytes=64)
+            nc.sync.dma_start(
+                rows[:], w[e, o * K_PASS : (o + 1) * K_PASS, n0 : n0 + width].rearrange("(p j) n -> p j n", j=PACK)
+            )
+            for at in range(0, width, HALF):
+                raw[e, o, (n0 + at) // HALF] = (rows, at)
 
-        y_sb = [keep.tile([P, S], F32, name="y_sb%d" % r, align_bytes=64) for r in range(TILES)]
+        def load_first_half_gate(k):
+            r, g = divmod(k, 2)
+            rows = wide.tile([P, T], F32, name="gate_sb", tag="load", align_bytes=64)
+            nc.sync.dma_start(rows[:], gate[g, r * P : (r + 1) * P, :])
+            gates[0, r, g] = [(0, T, rows[:])]
+
+        def load_second_half_gate(pool, t0, t1):
+            rows = pool.tile([P, 2, 2, t1 - t0], F32, name="gate_sb", tag="load", align_bytes=64)
+            for g in range(2):
+                nc.sync.dma_start(rows[:, g, :, :], gate[g, HALF:, t0:t1].rearrange("(r p) t -> p r t", p=P))
+                for r in range(2):
+                    gates.setdefault((1, r, g), []).append((t0, t1, rows[:, g, r, :]))
+
+        load_words(0)
+        for q in range(4):
+            nc.sync.dma_start(
+                xs_sb[32 * q : 32 * q + 4 * PASSES, :].bitcast(I32), x_scales[:, 4 * q : 4 * q + 4, :].bitcast(I32)
+            )
+        nc.sync.dma_start(offs_sb[:], offs)
+        load_words(1)
+        load_weights(wide, 0, 0, 0, N)
+        nc.sync.dma_start(pos_sb[0][:], pos1)
+        nc.sync.dma_start(pos_sb[1][:], pos2)
+        for e, o in [(e, o) for e in range(WHOLE) for o in range(PASSES)][1:]:
+            load_weights(wide, e, o, 0, N)
+        late = [(e, o) for e in range(WHOLE, E) for o in range(PASSES)]
+        for e, o in late:
+            load_weights(narrow, e, o, 0, HALF)
+        for k, (e, o) in enumerate(late[:-1]):
+            load_first_half_gate(k)
+            load_weights(narrow, e, o, HALF, HALF)
+        load_weights(narrow, *late[-1], HALF, HALF)
+        load_first_half_gate(len(late) - 1)
+        load_second_half_gate(narrow, 0, GATE_CUT)
+        wp_raw = keep.tile([P, PACK, M], F32, name="wp_raw", align_bytes=64)
+        nc.sync.dma_start(wp_raw[:], wp.rearrange("(p j) f -> p j f", j=PACK))
+        load_second_half_gate(wide, GATE_CUT, T)
+
+        tokens = {}
         grouped = {}
         codes = {}
+        y_sb = [keep.tile([P, SLOTS], F32, name="y_sb%d" % r, align_bytes=64) for r in range(N // P)]
+        products = {}
+        c_rows = {}
+        results = [keep.tile([P, M // P, width], F32, name="res%d" % t0, align_bytes=64) for t0, width in CHUNKS[1]]
 
-        def cast(key, engine, raw, at, width):
-            grouped[key] = ring([P, width, PACK], BF16, "grouped")
-            interleave(mover[engine], grouped[key][:], raw, at, at + width)
+        def gather_tokens(i):
+            pair, sort = i // 3, (0, SCALES, 1)[i % 3]
+            entries = offs_sb[:, pair * GATHER // STRIPE : (pair + 1) * GATHER // STRIPE]
+            if sort == SCALES:
+                tokens[pair, sort] = ring([P, GATHER], U8, "xsg")
+                nc.vector.tensor_copy(tokens[pair, sort][:], xs_sb[:].indirect(entries))
+            else:
+                tokens[pair, sort] = ring([P, GATHER], U32, "xg")
+                nc.vector.tensor_copy(tokens[pair, sort][:], x_sb[sort][:].bitcast(U32).indirect(entries))
 
-        def quantise(key, source, width):
+        def round_weights(key, copy, rows, at, width):
+            grouped[key] = ring([P, width * PACK], BF16, "grouped")
+            copy(
+                out=grouped[key][:].rearrange("p (c i j) -> p c j i", i=4, j=PACK),
+                in_=rows[:, :, at : at + width].rearrange("p j (c i) -> p c j i", i=4),
+            )
+
+        def quantise(key):
+            width = grouped[key].shape[1] // PACK
             words = ring([P, width], U32, "wq")
-            scales = small.tile([P, width], U8, name="ws", align_bytes=64)
-            nc.vector.quantize_mx(out=words[:].bitcast(FP8X4), scales=scales[:], in_=source)
+            scales = planes.tile([P, width], U8, name="ws", align_bytes=64)
+            nc.vector.quantize_mx(out=words[:].bitcast(FP8X4), scales=scales[:], in_=grouped[key][:])
             codes[key] = (words, scales)
 
-        sums = {}
+        def parts(piece):
+            if piece in CLOSING:
+                return [(piece + (r,), r * P, P) for r in range(2)]
+            return [(piece, 0, HALF)]
 
         def multiply(e, h, r):
-            b, s0 = divmod(e * C, GATHER)
-            acc = psum.tile([P, C], F32, name="acc", tag="bank")
+            pair, s0 = divmod(e * C, GATHER)
+            acc = bank([P, C], "acc")
             for o in range(PASSES):
-                words, scales = codes[e, o, h]
+                key, first = [(key, first) for key, first, width in parts((e, o, h)) if first <= r * P][-1]
+                words, scales = codes[key]
+                cols = slice(r * P - first, (r + 1) * P - first)
                 nc.tensor.matmul_mx(
                     out=acc[:],
-                    lhsT=words[:, r * P : (r + 1) * P].bitcast(FP8X4),
-                    lhsT_scale=scales[:, r * P : (r + 1) * P],
-                    rhs=xg[b, o][:, s0 : s0 + C].bitcast(FP8X4),
-                    rhs_scale=xg[b, PASSES][4 * o :, s0 : s0 + C],
+                    lhsT=words[:, cols].bitcast(FP8X4),
+                    lhsT_scale=scales[:, cols],
+                    rhs=tokens[pair, o][:, s0 : s0 + C].bitcast(FP8X4),
+                    rhs_scale=tokens[pair, SCALES][4 * o :, s0 : s0 + C],
                     start=(o == 0),
                     stop=(o == PASSES - 1),
                 )
-            sums["y", e, h, r] = acc
+            return (y_sb[2 * h + r][:, e * C : (e + 1) * C], acc)
 
-        def unload(e, h, r, engine):
-            mover[engine](out=y_sb[2 * h + r][:, e * C : (e + 1) * C], in_=sums["y", e, h, r][:])
+        def unload(target, acc):
+            on_scalar(out=target, in_=acc[:])
 
-        cb = {}
-        prods = {}
-
-        def combine_gather(h, t0, width, k):
+        def combine_gather(h, chunk, k):
+            t0, width = CHUNKS[h][chunk]
             r, g = divmod(k, 2)
-            prods[h, t0, k] = ring([P, width], F32, "prod")
-            b, at = divmod(t0, GATE_W)
+            start, rows = [(a, rows) for a, b, rows in gates[h, r, g] if a <= t0 < b][0]
+            products[h, t0, k] = ring([P, width], F32, "prod")
             nc.vector.tensor_tensor(
-                prods[h, t0, k][:],
-                y_sb[2 * h + r][:].indirect(pos_sb[g][:, t0 // 16 : (t0 + width) // 16]),
-                gates[h, b][:, g, r, at : at + width],
-                MULT,
+                products[h, t0, k][:],
+                y_sb[2 * h + r][:].indirect(pos_sb[g][:, t0 // STRIPE : (t0 + width) // STRIPE]),
+                rows[:, t0 - start : t0 - start + width],
+                mybir.AluOpType.mult,
             )
 
-        chunks = ([(b * GATE_W, GATE_W) for b in range(T // GATE_W)], list(zip(STARTS, LAST)))
-
-        def combine_sum(h, at):
-            t0 = max(s for s, width in chunks[h] if s <= at * P)
-            ct = psum.tile([P, HALF], F32, name="ct", tag="bank")
-            for k in range(4):
-                r, g = divmod(k, 2)
-                nc.tensor.matmul(
-                    ct[:, r * P : (r + 1) * P],
-                    lhsT=prods[h, t0, k][:, at * P - t0 : (at + 1) * P - t0],
-                    rhs=ident[:],
-                    start=(g == 0),
-                    stop=(g == 1),
-                    is_transpose=True,
+        def combine_sum(h, chunk, copy):
+            t0, width = CHUNKS[h][chunk]
+            for at in range(0, width, P):
+                summed = bank([P, HALF], "ct")
+                for k in range(4):
+                    r, g = divmod(k, 2)
+                    nc.tensor.matmul(
+                        summed[:, r * P : (r + 1) * P],
+                        lhsT=products[h, t0, k][:, at : at + P],
+                        rhs=ident[:],
+                        start=(g == 0),
+                        stop=(g == 1),
+                        is_transpose=True,
+                    )
+                block = (t0 + at) // P
+                if h == 0:
+                    c_rows[block] = ring([P, N], BF16, "cb")
+                in_half = slice(h * P // 2, (h + 1) * P // 2)
+                copy(
+                    out=c_rows[block][:].rearrange("t (u p e) -> t u p e", u=2, e=2)[:, :, in_half, :],
+                    in_=summed[:].rearrange("t (p u e) -> t u p e", u=2, e=2),
                 )
-            sums["c", h, at] = ct
 
-        def round_sum(h, at, engine):
-            if at not in cb:
-                cb[at] = ring([P, N], BF16, "cb")
-            mover[engine](
-                out=cb[at][:].rearrange("t (u p e) -> t u p e", u=2, e=2)[:, :, h * 64 : (h + 1) * 64, :],
-                in_=sums["c", h, at][:].rearrange("t (p u e) -> t u p e", u=2, e=2),
-            )
-
-        def turn(c):
-            t0, width = STARTS[c], LAST[c]
-            blocks = width // P
-            turned = psum.tile([P, blocks, 2, P], F32, name="turned", tag="bank")
-            for blk in range(blocks):
-                words = cb[t0 // P + blk][:].bitcast(F32)
+        def turn_back(chunk, copy):
+            t0, width = CHUNKS[1][chunk]
+            turned = bank([P, width // P, 2, P], "turned")
+            for b in range(width // P):
+                pairs = c_rows[t0 // P + b][:].bitcast(F32)
                 for u in range(2):
-                    nc.tensor.transpose(turned[:, blk, u, :], words[:, u * P : (u + 1) * P], ident[:])
-            sums["t", c] = turned
-
-        def unturn(c, engine):
-            grouped["c", c] = ring([P, LAST[c] * PACK], BF16, "cg")
-            mover[engine](
-                out=grouped["c", c][:].bitcast(F32).rearrange("p (b t u) -> p b t u", t=P, u=2),
-                in_=sums["t", c][:].rearrange("p b u t -> p b t u"),
+                    nc.tensor.transpose(turned[:, b, u, :], pairs[:, u * P : (u + 1) * P], ident[:])
+            grouped["c", chunk] = ring([P, width * PACK], BF16, "cg")
+            copy(
+                out=grouped["c", chunk][:].bitcast(F32).rearrange("p (b t u) -> p b t u", t=P, u=2),
+                in_=turned[:].rearrange("p b u t -> p b t u"),
             )
 
-        def project(c, part):
-            width = LAST[c]
-            cq, cs = codes["c", c]
-            first = 2 * part
-            count = min(M // P - first, 512 // width)
-            acc2 = psum.tile([P, count, width], F32, name="acc2", tag="bank")
-            for f in range(first, first + count):
-                words, scales = codes["wp", f // 2]
+        def project(chunk, f0, f1, copy):
+            words, scales = codes["c", chunk]
+            acc = bank([P, f1 - f0, CHUNKS[1][chunk][1]], "acc2")
+            for f in range(f0, f1):
+                wp_words, wp_scales = codes["wp", f // 2]
                 cols = slice(f % 2 * P, (f % 2 + 1) * P)
                 nc.tensor.matmul_mx(
-                    out=acc2[:, f - first, :],
-                    lhsT=words[:, cols].bitcast(FP8X4),
-                    lhsT_scale=scales[:, cols],
-                    rhs=cq[:].bitcast(FP8X4),
-                    rhs_scale=cs[:],
+                    out=acc[:, f - f0, :],
+                    lhsT=wp_words[:, cols].bitcast(FP8X4),
+                    lhsT_scale=wp_scales[:, cols],
+                    rhs=words[:].bitcast(FP8X4),
+                    rhs_scale=scales[:],
                     start=True,
                     stop=True,
                 )
-            sums["p", c, part] = (acc2, first, count)
+            copy(out=results[chunk][:, f0:f1, :], in_=acc[:])
 
-        res = [keep.tile([P, M // P, width], F32, name="res%d" % c, align_bytes=64) for c, width in enumerate(LAST)]
-        wp_parts = ((0, 256), (256, M - 256))
-        for word in SCRIPT.split():
-            kind, engine = word[0], word[-1]
-            a = [int(ch) for ch in word[1:] if ch in "0123456789"]
-            if word[:2] == "cw":
-                cast(("wp", a[0]), engine, wp_raw, *wp_parts[a[0]])
-            elif word[:2] == "qw":
-                quantise(("wp", a[0]), grouped["wp", a[0]][:].rearrange("p w j -> p (w j)"), wp_parts[a[0]][1])
-            elif word[:2] == "qc":
-                quantise(("c", a[0]), grouped["c", a[0]][:], LAST[a[0]])
-            elif kind == "c":
-                cast(tuple(a), engine, *pieces[tuple(a)], HALF)
-            elif kind == "q":
-                quantise(tuple(a), grouped[tuple(a)][:].rearrange("p w j -> p (w j)"), HALF)
-            elif kind == "x":
-                gather_tokens(*a)
-            elif kind == "m":
-                multiply(*a)
-            elif kind == "y":
-                unload(*a, engine)
-            elif kind == "g":
-                combine_gather(a[0], *chunks[a[0]][a[1]], a[2])
-            elif kind == "s":
-                combine_sum(*a)
-            elif kind == "e":
-                round_sum(*a, engine)
-            elif kind == "t":
-                turn(*a)
-            elif kind == "u":
-                unturn(*a, engine)
-            elif kind == "p":
-                project(a[0], "ab".index(word[2]))
-            elif kind == "r":
-                acc2, first, count = sums["p", a[0], "ab".index(word[2])]
-                mover[engine](out=res[a[0]][:, first : first + count, :], in_=acc2[:])
-            else:
-                t0, width = chunks[1][a[0]]
-                nc.sync.dma_start(out[:, t0 : t0 + width].rearrange("(f p) t -> p f t", p=P), res[a[0]][:])
+        def store(chunk, f0, f1):
+            t0, width = CHUNKS[1][chunk]
+            nc.sync.dma_start(
+                out[f0 * P : f1 * P, t0 : t0 + width].rearrange("(f p) t -> p f t", p=P), results[chunk][:, f0:f1, :]
+            )
+
+        first_half = [(chunk, k) for k in range(4) for chunk in range(len(CHUNKS[0]))]
+        filled = []
+        for step in range(-1, len(PIECES)):
+            if step >= 0:
+                rows, at = raw[PIECES[step]]
+                for key, first, width in parts(PIECES[step]):
+                    round_weights(key, on_vector if step in ON_VECTOR else on_scalar, rows, at + first, width)
+            for target, acc in filled:
+                unload(target, acc)
+            filled = []
+            for i in range(len(TOKEN_GATHER_AT)):
+                if TOKEN_GATHER_AT[i] == step:
+                    gather_tokens(i)
+            count = FIRST_HALF_GATHERS.get(step, 0)
+            for chunk, k in first_half[:count]:
+                combine_gather(0, chunk, k)
+            first_half = first_half[count:]
+            due = [PIECES[step - 1]] if step >= 1 and PIECES[step - 1] not in CLOSING else []
+            due += [PIECES[step]] if step >= 0 and PIECES[step] in CLOSING else []
+            for piece in due:
+                for key, first, width in parts(piece):
+                    quantise(key)
+            for e, o, h in due:
+                if o == PASSES - 1:
+                    for r in range(2):
+                        filled.append(multiply(e, h, r))
+                        if (e, o, h) in CLOSING:
+                            unload(*filled.pop())
+        for chunk, k in first_half:
+            combine_gather(0, chunk, k)
+        for chunk in range(len(CHUNKS[0])):
+            combine_sum(0, chunk, on_scalar)
+        for i, (f0, width) in enumerate(WP_PARTS):
+            round_weights(("wp", i), on_scalar, wp_raw, f0, width)
+
+        def gather_chunk(chunk):
+            for k in range(4):
+                combine_gather(1, chunk, k)
+
+        gather_chunk(0)
+        combine_sum(1, 0, on_scalar)
+        turn_back(0, on_scalar)
+        gather_chunk(1)
+        combine_sum(1, 1, on_scalar)
+        gather_chunk(2)
+        for i in range(len(WP_PARTS)):
+            quantise(("wp", i))
+        quantise(("c", 0))
+        combine_sum(1, 2, on_scalar)
+        turn_back(1, on_scalar)
+        project(0, 0, 2, on_scalar)
+        project(0, 2, 3, on_scalar)
+        store(0, 0, 3)
+        gather_chunk(3)
+        quantise(("c", 1))
+        turn_back(2, on_vector)
+        combine_sum(1, 3, on_vector)
+        quantise(("c", 2))
+        project(1, 0, 2, on_vector)
+        project(1, 2, 3, on_scalar)
+        store(1, 0, 3)
+        turn_back(3, on_scalar)
+        project(2, 0, 3, on_scalar)
+        store(2, 0, 3)
+        quantise(("c", 3))
+        for f, copy in enumerate((on_scalar, on_vector, on_scalar)):
+            project(3, f, f + 1, copy)
+            store(3, f, f + 1)

@@ -29,11 +29,11 @@ PIECES = [(e, o, h) for e in range(WHOLE) for o in range(PASSES) for h in range(
     (e, o, h) for h in range(2) for e in range(WHOLE, E) for o in range(PASSES)
 ]
 CLOSING = [(E - 1, PASSES - 1, h) for h in range(2)]
-ON_VECTOR = (4, 6, 9, 12, 14, 16, 18)
-TOKEN_GATHER_AT = (-1, 0, 1, 1, 2, 3, 5, 8, 11)
+ON_VECTOR = [PIECES[i] for i in (4, 6, 9, 12, 14, 16, 18)] + [CLOSING[1] + (0,)]
+TOKEN_GATHER_AT = (-1, -1, 0, 1, 2, 3, 5, 8, 11)
 FIRST_HALF_GATHERS = {21: 4, 22: 5}
 CHUNKS = ([(0, 256), (256, 256), (512, 256)], [(0, 256), (256, 256), (512, 128), (640, 128)])
-GATE_CUT = 256
+GATE_TOKENS = 256
 WP_PARTS = ((0, 256), (256, 128))
 RING = 40
 PLANES = 12
@@ -63,7 +63,7 @@ def tile_moe_nxt_lin_none_kernel(tc, x_words, x_scales, w, wp, gate, offs, pos1,
         xs_sb = keep.tile([P, T], U8, name="xs_sb", align_bytes=64)
         ident = keep.tile([P, P], F32, name="ident", align_bytes=64)
 
-        nc.vector.memset(xs_sb[:].bitcast(I32), 0)
+        nc.gpsimd.memset(xs_sb[:].bitcast(I32), 0)
         make_identity(nc, ident[:])
 
         raw = {}
@@ -86,25 +86,26 @@ def tile_moe_nxt_lin_none_kernel(tc, x_words, x_scales, w, wp, gate, offs, pos1,
             nc.sync.dma_start(rows[:], gate[g, r * P : (r + 1) * P, :])
             gates[0, r, g] = [(0, T, rows[:])]
 
-        def load_second_half_gate(pool, t0, t1):
-            rows = pool.tile([P, 2, 2, t1 - t0], F32, name="gate_sb", tag="load", align_bytes=64)
+        def load_second_half_gate(t0):
+            t1 = t0 + GATE_TOKENS
+            rows = narrow.tile([P, 2, 2, GATE_TOKENS], F32, name="gate_sb", tag="load", align_bytes=64)
             for g in range(2):
                 nc.sync.dma_start(rows[:, g, :, :], gate[g, HALF:, t0:t1].rearrange("(r p) t -> p r t", p=P))
                 for r in range(2):
                     gates.setdefault((1, r, g), []).append((t0, t1, rows[:, g, r, :]))
 
         load_words(0)
+        nc.sync.dma_start(offs_sb[:], offs)
+        load_words(1)
         for q in range(4):
             nc.sync.dma_start(
                 xs_sb[32 * q : 32 * q + 4 * PASSES, :].bitcast(I32), x_scales[:, 4 * q : 4 * q + 4, :].bitcast(I32)
             )
-        nc.sync.dma_start(offs_sb[:], offs)
-        load_words(1)
-        load_weights(wide, 0, 0, 0, N)
+        for e in range(WHOLE):
+            for o in range(PASSES):
+                load_weights(wide, e, o, 0, N)
         nc.sync.dma_start(pos_sb[0][:], pos1)
         nc.sync.dma_start(pos_sb[1][:], pos2)
-        for e, o in [(e, o) for e in range(WHOLE) for o in range(PASSES)][1:]:
-            load_weights(wide, e, o, 0, N)
         late = [(e, o) for e in range(WHOLE, E) for o in range(PASSES)]
         for e, o in late:
             load_weights(narrow, e, o, 0, HALF)
@@ -113,10 +114,11 @@ def tile_moe_nxt_lin_none_kernel(tc, x_words, x_scales, w, wp, gate, offs, pos1,
             load_weights(narrow, e, o, HALF, HALF)
         load_weights(narrow, *late[-1], HALF, HALF)
         load_first_half_gate(len(late) - 1)
-        load_second_half_gate(narrow, 0, GATE_CUT)
+        load_second_half_gate(0)
         wp_raw = keep.tile([P, PACK, M], F32, name="wp_raw", align_bytes=64)
         nc.sync.dma_start(wp_raw[:], wp.rearrange("(p j) f -> p j f", j=PACK))
-        load_second_half_gate(wide, GATE_CUT, T)
+        for t0 in range(GATE_TOKENS, T, GATE_TOKENS):
+            load_second_half_gate(t0)
 
         tokens = {}
         grouped = {}
@@ -127,7 +129,7 @@ def tile_moe_nxt_lin_none_kernel(tc, x_words, x_scales, w, wp, gate, offs, pos1,
         results = [keep.tile([P, M // P, width], F32, name="res%d" % t0, align_bytes=64) for t0, width in CHUNKS[1]]
 
         def gather_tokens(i):
-            pair, sort = i // 3, (0, SCALES, 1)[i % 3]
+            pair, sort = i // 3, (0, 1, SCALES)[i % 3]
             entries = offs_sb[:, pair * GATHER // STRIPE : (pair + 1) * GATHER // STRIPE]
             if sort == SCALES:
                 tokens[pair, sort] = ring([P, GATHER], U8, "xsg")
@@ -253,7 +255,7 @@ def tile_moe_nxt_lin_none_kernel(tc, x_words, x_scales, w, wp, gate, offs, pos1,
             if step >= 0:
                 rows, at = raw[PIECES[step]]
                 for key, first, width in parts(PIECES[step]):
-                    round_weights(key, on_vector if step in ON_VECTOR else on_scalar, rows, at + first, width)
+                    round_weights(key, on_vector if key in ON_VECTOR else on_scalar, rows, at + first, width)
             for target, acc in filled:
                 unload(target, acc)
             filled = []
@@ -279,8 +281,6 @@ def tile_moe_nxt_lin_none_kernel(tc, x_words, x_scales, w, wp, gate, offs, pos1,
             combine_gather(0, chunk, k)
         for chunk in range(len(CHUNKS[0])):
             combine_sum(0, chunk, on_scalar)
-        for i, (f0, width) in enumerate(WP_PARTS):
-            round_weights(("wp", i), on_scalar, wp_raw, f0, width)
 
         def gather_chunk(chunk):
             for k in range(4):
@@ -288,6 +288,8 @@ def tile_moe_nxt_lin_none_kernel(tc, x_words, x_scales, w, wp, gate, offs, pos1,
 
         gather_chunk(0)
         combine_sum(1, 0, on_scalar)
+        for i, (f0, width) in enumerate(WP_PARTS):
+            round_weights(("wp", i), on_scalar, wp_raw, f0, width)
         turn_back(0, on_scalar)
         gather_chunk(1)
         combine_sum(1, 1, on_scalar)

from contextlib import ExitStack

import concourse.mybir as mybir
from concourse.masks import make_identity

K, T, E, C, N, M = 1024, 768, 6, 256, 512, 384
SLOTS = E * C
FLOPS = 2 * K * N * SLOTS + 2 * N * M * T

F32 = mybir.dt.float32
BF16 = mybir.dt.bfloat16
I32 = mybir.dt.int32
U32 = mybir.dt.uint32
U16 = mybir.dt.uint16
U8 = mybir.dt.uint8
FP8X4 = mybir.dt.float8_e4m3fn_x4

P = 128
PACK = 4
K_PASS = P * PACK
PASSES = K // K_PASS
HALF = N // 2
STRIPE = 16
GATHER = 512
SCALES = PASSES
WHOLE = 4

PIECES = [(e, o, h) for e in range(WHOLE) for o in range(PASSES) for h in range(2)] + [
    (e, o, h) for h in range(2) for e in range(WHOLE, E) for o in range(PASSES)
]
CLOSING = [(E - 1, PASSES - 1, h) for h in range(2)]
ON_VECTOR = [PIECES[i] for i in (4, 6, 9, 12, 14, 16, 18)] + [CLOSING[1] + (0,)]
TOKEN_GATHER_AT = (-1, -1, 0, 1, 2, 3, 5, 8, 11)
FIRST_HALF_GATHERS = {21: 4, 22: 5}
CHUNKS = ([(0, 256), (256, 256), (512, 256)], [(0, 256), (256, 256), (512, 128), (640, 128)])
GATE_TOKENS = 256
WP_PARTS = ((0, 256), (256, 128))
RING = 40
PLANES = 12


def tile_moe_nxt_lin_none_kernel(tc, x_words, x_scales, w, wp, gate, offs, pos1, pos2, out):
    nc = tc.nc
    on_scalar, on_vector = nc.scalar.copy, nc.vector.tensor_copy
    with ExitStack() as ctx:
        lists = ctx.enter_context(tc.tile_pool(name="lists", bufs=1))
        keep = ctx.enter_context(tc.tile_pool(name="keep", bufs=1))
        wide = ctx.enter_context(tc.tile_pool(name="wide", bufs=WHOLE * PASSES))
        narrow = ctx.enter_context(tc.tile_pool(name="narrow", bufs=(E - WHOLE) * PASSES * 2))
        ring_pool = ctx.enter_context(tc.tile_pool(name="ring", bufs=RING))
        planes = ctx.enter_context(tc.tile_pool(name="planes", bufs=PLANES))
        psum = ctx.enter_context(tc.psum_pool(name="psum", bufs=8))

        def ring(shape, dtype, name):
            return ring_pool.tile(shape, dtype, name=name, tag="ring", align_bytes=64)

        def bank(shape, name):
            return psum.tile(shape, F32, name=name, tag="bank")

        offs_sb = lists.tile([P, SLOTS // STRIPE], U16, name="offs_sb")
        pos_sb = [lists.tile([P, T // STRIPE], U16, name="pos_sb%d" % g) for g in range(2)]
        x_sb = [keep.tile([P, T], I32, name="x_sb%d" % o, align_bytes=64) for o in range(PASSES)]
        xs_sb = keep.tile([P, T], U8, name="xs_sb", align_bytes=64)
        ident = keep.tile([P, P], F32, name="ident", align_bytes=64)

        nc.gpsimd.memset(xs_sb[:].bitcast(I32), 0)
        make_identity(nc, ident[:])

        raw = {}
        gates = {}

        def load_words(o):
            nc.sync.dma_start(x_sb[o][:], x_words[o].rearrange("p t r -> p (t r)").bitcast(I32))

        def load_weights(pool, e, o, n0, width):
            rows = pool.tile([P, PACK, width], F32, name="raw", tag="load", align_bytes=64)
            nc.sync.dma_start(
                rows[:], w[e, o * K_PASS : (o + 1) * K_PASS, n0 : n0 + width].rearrange("(p j) n -> p j n", j=PACK)
            )
            for at in range(0, width, HALF):
                raw[e, o, (n0 + at) // HALF] = (rows, at)

        def load_first_half_gate(k):
            r, g = divmod(k, 2)
            rows = wide.tile([P, T], F32, name="gate_sb", tag="load", align_bytes=64)
            nc.sync.dma_start(rows[:], gate[g, r * P : (r + 1) * P, :])
            gates[0, r, g] = [(0, T, rows[:])]

        def load_second_half_gate(t0):
            t1 = t0 + GATE_TOKENS
            rows = narrow.tile([P, 2, 2, GATE_TOKENS], F32, name="gate_sb", tag="load", align_bytes=64)
            for g in range(2):
                nc.sync.dma_start(rows[:, g, :, :], gate[g, HALF:, t0:t1].rearrange("(r p) t -> p r t", p=P))
                for r in range(2):
                    gates.setdefault((1, r, g), []).append((t0, t1, rows[:, g, r, :]))

        load_words(0)
        nc.sync.dma_start(offs_sb[:], offs)
        load_words(1)
        for q in range(4):
            nc.sync.dma_start(
                xs_sb[32 * q : 32 * q + 4 * PASSES, :].bitcast(I32), x_scales[:, 4 * q : 4 * q + 4, :].bitcast(I32)
            )
        for e in range(WHOLE):
            for o in range(PASSES):
                load_weights(wide, e, o, 0, N)
        nc.sync.dma_start(pos_sb[0][:], pos1)
        nc.sync.dma_start(pos_sb[1][:], pos2)
        late = [(e, o) for e in range(WHOLE, E) for o in range(PASSES)]
        for e, o in late:
            load_weights(narrow, e, o, 0, HALF)
        for k, (e, o) in enumerate(late[:-1]):
            load_first_half_gate(k)
            load_weights(narrow, e, o, HALF, HALF)
        load_weights(narrow, *late[-1], HALF, HALF)
        load_first_half_gate(len(late) - 1)
        load_second_half_gate(0)
        wp_raw = keep.tile([P, PACK, M], F32, name="wp_raw", align_bytes=64)
        nc.sync.dma_start(wp_raw[:], wp.rearrange("(p j) f -> p j f", j=PACK))
        for t0 in range(GATE_TOKENS, T, GATE_TOKENS):
            load_second_half_gate(t0)

        tokens = {}
        grouped = {}
        codes = {}
        y_sb = [keep.tile([P, SLOTS], F32, name="y_sb%d" % r, align_bytes=64) for r in range(N // P)]
        products = {}
        c_rows = {}
        results = [keep.tile([P, M // P, width], F32, name="res%d" % t0, align_bytes=64) for t0, width in CHUNKS[1]]

        def gather_tokens(i):
            pair, sort = i // 3, (0, 1, SCALES)[i % 3]
            entries = offs_sb[:, pair * GATHER // STRIPE : (pair + 1) * GATHER // STRIPE]
            if sort == SCALES:
                tokens[pair, sort] = ring([P, GATHER], U8, "xsg")
                nc.vector.tensor_copy(tokens[pair, sort][:], xs_sb[:].indirect(entries))
            else:
                tokens[pair, sort] = ring([P, GATHER], U32, "xg")
                nc.vector.tensor_copy(tokens[pair, sort][:], x_sb[sort][:].bitcast(U32).indirect(entries))

        def round_weights(key, copy, rows, at, width):
            grouped[key] = ring([P, width * PACK], BF16, "grouped")
            copy(
                out=grouped[key][:].rearrange("p (c i j) -> p c j i", i=4, j=PACK),
                in_=rows[:, :, at : at + width].rearrange("p j (c i) -> p c j i", i=4),
            )

        def quantise(key):
            width = grouped[key].shape[1] // PACK
            words = ring([P, width], U32, "wq")
            scales = planes.tile([P, width], U8, name="ws", align_bytes=64)
            nc.vector.quantize_mx(out=words[:].bitcast(FP8X4), scales=scales[:], in_=grouped[key][:])
            codes[key] = (words, scales)

        def parts(piece):
            if piece in CLOSING:
                return [(piece + (r,), r * P, P) for r in range(2)]
            return [(piece, 0, HALF)]

        def multiply(e, h, r):
            pair, s0 = divmod(e * C, GATHER)
            acc = bank([P, C], "acc")
            for o in range(PASSES):
                key, first = [(key, first) for key, first, width in parts((e, o, h)) if first <= r * P][-1]
                words, scales = codes[key]
                cols = slice(r * P - first, (r + 1) * P - first)
                nc.tensor.matmul_mx(
                    out=acc[:],
                    lhsT=words[:, cols].bitcast(FP8X4),
                    lhsT_scale=scales[:, cols],
                    rhs=tokens[pair, o][:, s0 : s0 + C].bitcast(FP8X4),
                    rhs_scale=tokens[pair, SCALES][4 * o :, s0 : s0 + C],
                    start=(o == 0),
                    stop=(o == PASSES - 1),
                )
            return (y_sb[2 * h + r][:, e * C : (e + 1) * C], acc)

        def unload(target, acc):
            on_scalar(out=target, in_=acc[:])

        def combine_gather(h, chunk, k):
            t0, width = CHUNKS[h][chunk]
            r, g = divmod(k, 2)
            start, rows = [(a, rows) for a, b, rows in gates[h, r, g] if a <= t0 < b][0]
            products[h, t0, k] = ring([P, width], F32, "prod")
            nc.vector.tensor_tensor(
                products[h, t0, k][:],
                y_sb[2 * h + r][:].indirect(pos_sb[g][:, t0 // STRIPE : (t0 + width) // STRIPE]),
                rows[:, t0 - start : t0 - start + width],
                mybir.AluOpType.mult,
            )

        def combine_sum(h, chunk, copy):
            t0, width = CHUNKS[h][chunk]
            for at in range(0, width, P):
                summed = bank([P, HALF], "ct")
                for k in range(4):
                    r, g = divmod(k, 2)
                    nc.tensor.matmul(
                        summed[:, r * P : (r + 1) * P],
                        lhsT=products[h, t0, k][:, at : at + P],
                        rhs=ident[:],
                        start=(g == 0),
                        stop=(g == 1),
                        is_transpose=True,
                    )
                block = (t0 + at) // P
                if h == 0:
                    c_rows[block] = ring([P, N], BF16, "cb")
                in_half = slice(h * P // 2, (h + 1) * P // 2)
                copy(
                    out=c_rows[block][:].rearrange("t (u p e) -> t u p e", u=2, e=2)[:, :, in_half, :],
                    in_=summed[:].rearrange("t (p u e) -> t u p e", u=2, e=2),
                )

        def turn_back(chunk, copy):
            t0, width = CHUNKS[1][chunk]
            turned = bank([P, width // P, 2, P], "turned")
            for b in range(width // P):
                pairs = c_rows[t0 // P + b][:].bitcast(F32)
                for u in range(2):
                    nc.tensor.transpose(turned[:, b, u, :], pairs[:, u * P : (u + 1) * P], ident[:])
            grouped["c", chunk] = ring([P, width * PACK], BF16, "cg")
            copy(
                out=grouped["c", chunk][:].bitcast(F32).rearrange("p (b t u) -> p b t u", t=P, u=2),
                in_=turned[:].rearrange("p b u t -> p b t u"),
            )

        def project(chunk, f0, f1, copy):
            words, scales = codes["c", chunk]
            acc = bank([P, f1 - f0, CHUNKS[1][chunk][1]], "acc2")
            for f in range(f0, f1):
                wp_words, wp_scales = codes["wp", f // 2]
                cols = slice(f % 2 * P, (f % 2 + 1) * P)
                nc.tensor.matmul_mx(
                    out=acc[:, f - f0, :],
                    lhsT=wp_words[:, cols].bitcast(FP8X4),
                    lhsT_scale=wp_scales[:, cols],
                    rhs=words[:].bitcast(FP8X4),
                    rhs_scale=scales[:],
                    start=True,
                    stop=True,
                )
            copy(out=results[chunk][:, f0:f1, :], in_=acc[:])

        def store(chunk, f0, f1):
            t0, width = CHUNKS[1][chunk]
            nc.sync.dma_start(
                out[f0 * P : f1 * P, t0 : t0 + width].rearrange("(f p) t -> p f t", p=P), results[chunk][:, f0:f1, :]
            )

        first_half = [(chunk, k) for k in range(4) for chunk in range(len(CHUNKS[0]))]
        filled = []
        for step in range(-1, len(PIECES)):
            if step >= 0:
                rows, at = raw[PIECES[step]]
                for key, first, width in parts(PIECES[step]):
                    round_weights(key, on_vector if key in ON_VECTOR else on_scalar, rows, at + first, width)
            for target, acc in filled:
                unload(target, acc)
            filled = []
            for i in range(len(TOKEN_GATHER_AT)):
                if TOKEN_GATHER_AT[i] == step:
                    gather_tokens(i)
            count = FIRST_HALF_GATHERS.get(step, 0)
            for chunk, k in first_half[:count]:
                combine_gather(0, chunk, k)
            first_half = first_half[count:]
            due = [PIECES[step - 1]] if step >= 1 and PIECES[step - 1] not in CLOSING else []
            due += [PIECES[step]] if step >= 0 and PIECES[step] in CLOSING else []
            for piece in due:
                for key, first, width in parts(piece):
                    quantise(key)
            for e, o, h in due:
                if o == PASSES - 1:
                    for r in range(2):
                        filled.append(multiply(e, h, r))
                        if (e, o, h) in CLOSING:
                            unload(*filled.pop())
        for chunk, k in first_half:
            combine_gather(0, chunk, k)
        for chunk in range(len(CHUNKS[0])):
            combine_sum(0, chunk, on_scalar)

        def gather_chunk(chunk):
            for k in range(4):
                combine_gather(1, chunk, k)

        gather_chunk(0)
        combine_sum(1, 0, on_scalar)
        for i, (f0, width) in enumerate(WP_PARTS):
            round_weights(("wp", i), on_scalar, wp_raw, f0, width)
        turn_back(0, on_scalar)
        gather_chunk(1)
        combine_sum(1, 1, on_scalar)
        gather_chunk(2)
        for i in range(len(WP_PARTS)):
            quantise(("wp", i))
        quantise(("c", 0))
        combine_sum(1, 2, on_scalar)
        turn_back(1, on_scalar)
        project(0, 0, 2, on_scalar)
        project(0, 2, 3, on_scalar)
        store(0, 0, 3)
        gather_chunk(3)
        quantise(("c", 1))
        turn_back(2, on_vector)
        combine_sum(1, 3, on_vector)
        quantise(("c", 2))
        project(1, 0, 2, on_vector)
        project(1, 2, 3, on_scalar)
        store(1, 0, 3)
        turn_back(3, on_scalar)
        project(2, 0, 3, on_scalar)
        store(2, 0, 3)
        quantise(("c", 3))
        for f, copy in enumerate((on_scalar, on_vector, on_scalar)):
            project(3, f, f + 1, copy)
            store(3, f, f + 1)
